import numpy as np, ml_dtypes
CORES = [23,119,17,113]
N = 4
import mx_ref
BF = ml_dtypes.bfloat16
def gentries(a):
    return np.ascontiguousarray(a.reshape(8, 16, -1).transpose(0, 2, 1)).reshape(8, -1)
def gtable(e):
    e = np.asarray(e); return np.ascontiguousarray(e.reshape(8, -1, 16).transpose(0, 2, 1)).reshape(128, -1).astype(np.int32)
def gcols(t, e):
    v = np.concatenate([t.reshape(8, 16, -1, 4), np.zeros((8, 16, 1, 4), BF)], axis=2)
    return np.ascontiguousarray(np.stack([v[g][:, e[g]] for g in range(8)])).reshape(128, -1)
def tile(rs):
    return np.stack(rs, axis=2).reshape(128, -1).astype(BF)
def pick(q, e):
    c = np.concatenate([q[0].reshape(128, -1, 4), np.zeros((128, 1, 4), np.uint8)], axis=1); s = np.concatenate([q[1], np.ones((16, 1), np.uint8)], axis=1)
    return (np.ascontiguousarray(c[:, e].reshape(128, -1)), np.ascontiguousarray(s[:, e]))
def join(*qs):
    return (np.concatenate([q[0] for q in qs], axis=1), np.concatenate([q[1] for q in qs], axis=1))
def put(q, e, v):
    c, s = q[0].reshape(128, -1, 4).copy(), q[1].copy(); c[:, e] = v[0].reshape(128, -1, 4); s[:, e] = v[1]
    return (c.reshape(128, -1), s)
def pk(c, s):
    return (np.ascontiguousarray(c), mx_ref.live(s))
def emit(q):
    return q[0], q[1]
def packed(v, rng):
    q = [mx_ref.quantize(np.ascontiguousarray(v[r])) for r in range(N)]
    return np.stack([a for a, b in q]), np.stack([mx_ref.plane(b, rng) for a, b in q])
def values_of_codes():
    e, c = np.zeros((128, 128, 4), np.float32), np.zeros((128, 2, 4), np.uint8)
    e[np.arange(128), np.arange(128), 0] = 1
    c[:127, :, 0] = np.arange(256).reshape(2, 128).T[:127]
    return mx_ref.matmul(mx_ref.quantize(e.reshape(128, 512).astype(BF)), (c.reshape(128, 8), np.full((16, 2), 127, np.uint8))).T.reshape(-1).astype(np.float64)
CODE_VALUE, SCALE_VALUE = values_of_codes(), 2.0 ** (np.arange(256) - 127.0)
def decode(q):
    return (CODE_VALUE[q[0]].reshape(16, 8, -1, 4) * SCALE_VALUE[q[1]][:, None, :, None] + 0.0).reshape(128, -1).astype(np.float32)
def f(rng, *shape):
    return mx_ref.flush((rng.standard_normal(shape, dtype=np.float32) * np.exp2(rng.integers(-2, 3, shape[:-1] + (1,)))).astype(BF))
def wide(rng, *shape, cols=0):
    v = rng.standard_normal(shape, dtype=np.float32) * np.exp2(rng.integers(-12, 13, shape)).astype(np.float32)
    if cols: v *= np.repeat(np.exp2(rng.integers(-cols, cols + 1, shape[:-2] + (1, shape[-1] // 4))) * (rng.random(shape[:-2] + (1, shape[-1] // 4)) > 0.0625), 4, axis=-1).astype(np.float32)
    return mx_ref.flush(v.astype(BF))
C, H, E, R = 320, 96, 416, 3
def big(v):
    v = v.astype(np.float32)
    v[np.abs(v) < np.float32(2.0 ** -16)] = 0
    return v.astype(BF)
def numbers_of(rng):
    return {"x": big(f(rng, N, 128, 4 * C)), "u": np.array(f(rng, N, 128, 512)), "v": np.array(f(rng, N, 128, 512))}
def stored(a):
    return np.stack([gtable(a[r]) for r in range(N)])
def lists(rng):
    return {"lf": stored(rng.integers(0, E, (N, 8, E))), "rt": stored(rng.integers(0, E, (N, 8, E)))}
def layers(rng, still=[]):
    w = big(f(rng, N, 128, 2048)).reshape(N, 8, 16, 4, 8, 16, 4)
    for i in still:
        w[:, :, i] = 0
        w[:, :, :, :, :, i] = 0
    return w
def weights(rng, w):
    c, p = packed(np.ascontiguousarray(w).reshape(N, 128, 2048), rng)
    return {"wc": c, "ws": p}
def setup_inputs(rng):
    return {**numbers_of(rng), **lists(rng), **weights(rng, layers(rng))}
def setup_inputs_ties(rng):
    d = numbers_of(rng)
    o = rng.permutation(N)
    x = d["x"].reshape(N, 8, 16, C, 4)
    x[:, :, 0] = 0
    x[:, :, 0, :, 0] = rng.integers(-2, 3, (N, 8, C)).astype(np.float32).astype(BF)
    u = d["u"].reshape(N, 128, 128, 4)
    u[:, :, ::16] = 0
    for h in range(0, 128, 16): u[:, h, h, 0] = 1
    u[o[0], :, ::16] = 0
    e = lists(rng)
    e["rt"][o[1]] = e["lf"][o[1]]
    return {"x": x.reshape(N, 128, 4 * C), "u": u.reshape(N, 128, 512), "v": d["v"], **e, **weights(rng, layers(rng, [0]))}
def setup_inputs_near(rng):
    d = numbers_of(rng)
    kind = rng.permutation(8) % 4
    x = d["x"].astype(np.float32).reshape(N, 8, 16, C, 4)
    c = rng.integers(0, 2, (N, 8, C)) * 2.0 - 1.0
    s = rng.integers(0, 16, (N, 8, C))
    x[:, :, 0] = 0
    x[:, :, 8:] = 0
    x[:, :, 0, :, 0] = c
    x[:, :, 8] = c[:, :, :, None] * ((s[:, :, :, None] >> np.arange(4)) & 1) * np.exp2(np.arange(4) - 23.0)
    x[:, :, 11, :, 0] = c * 2.0 ** -10
    u = d["u"].reshape(N, 128, 128, 4)
    u[:, :, ::16] = 0
    for g in range(8):
        h, m = 16 * g, 1.0 if kind[g] == 0 else 2.0 ** -30
        if kind[g] < 2:
            u[:, h, h, 0] = m
            u[:, h + 11, h, 0] = m
        if kind[g] < 3: u[:, h + 8, h] = m
        else:
            a = rng.integers(0, 2, (N, C))
            x[:, g, 8:] = 0
            x[:, g, 10, :, 0] = c[:, g] * a * 1.125 * 2.0 ** -30
            x[:, g, 10, :, 1] = c[:, g] * (1 - a) * 1.25 * 2.0 ** -30
            u[:, h + 10, h, 0] = m * 1.125
            u[:, h + 10, h, 1] = m
    x = (x + np.float32(0.0)).reshape(N, 128, 4 * C).astype(BF)
    return {"x": x, "u": u.reshape(N, 128, 512), "v": d["v"], **lists(rng), **weights(rng, layers(rng, [0, 8, 9, 10, 11, 12, 13, 14, 15]))}
def setup_inputs_twice(rng):
    d = numbers_of(rng)
    x = (2 * rng.integers(0, 8, (N, 8, 16, C, 4)) + 1) * np.exp2(rng.integers(-17, -15, (N, 8, 16, C, 4))) * (rng.integers(0, 2, (N, 8, 16, C, 4)) * 2.0 - 1.0)
    x[:, :, ::8, :, 0] = np.where(rng.random((N, 8, 2, C)) < 0.5, 1.96875, 1.75) * (rng.integers(0, 2, (N, 8, 2, C)) * 2.0 - 1.0)
    a = int(rng.integers(1, 8))
    x[:, a, ::8, :, 0] = 1.75
    t = np.arange(C) % 4 == rng.integers(0, 4, (N, 1))
    x[:, 0] = np.where(t[:, None, :, None], 0.0, x[:, 0])
    x[:, 0, ::8, :, 0] = np.where(t[:, None], 1.75 * 2.0 ** -24 * (rng.integers(0, 2, (N, 2, C)) * 2.0 - 1.0), x[:, 0, ::8, :, 0])
    u = d["u"].reshape(N, 128, 128, 4)
    u[:, ::8, ::16] = 0
    w = np.zeros((N, 128, 4, 128, 4), np.float32)
    i = np.arange(128)
    for b in range(4): w[:, i, b, i, b] = -32
    w[:, i[::16], 0, i[::16], 0] = -36
    w[:, i[8::16], 0, i[8::16], 0] = -18
    w[:, :, :, :16] = 0
    w[:, :, :, 16 * a:16 * a + 16] = 0
    m = np.arange(16)
    k = np.where(np.arange(N) % 2 == rng.integers(0, 2), 1.0, -1.0)[:, None]
    for b in range(4): w[:, 16 * a + m, b, m, b] = 32 * k
    w[:, 16 * a + m[::8], 0, m[::8], 0] = 36 * k
    e = rng.integers(0, E, (2, N, 8, E))
    for r in range(N):
        e[:, r, 0, :C] = rng.permutation(np.concatenate([np.arange(H), np.arange(C, E), H + rng.permutation(C - H)[:C - 2 * H]]))
    return {"x": x.astype(np.float32).reshape(N, 128, 4 * C).astype(BF), "u": u.reshape(N, 128, 512), "v": d["v"], "lf": stored(e[0]), "rt": stored(e[1]), **weights(rng, w.astype(BF))}
def setup_inputs_ends(rng):
    d = numbers_of(rng)
    e = rng.permutation(N)
    h = rng.permutation(8)
    most = 1.34375 * 2.0 ** 28
    x = (0.6 + 0.4 * rng.random((N, 8, 16, C, 4))) * most
    x[e[::2]] = most
    c = rng.integers(0, 2, (N, 1, 1, C, 1)) * 2.0 - 1.0
    c[e[1]] = c[e[1], 0, 0, 0, 0]
    x = x * c
    x[:, h[4:], 8:] = (rng.integers(0, 2, (N, 4, 8, C, 4)) * 2.0 - 1.0) * 2.0 ** -30
    u = d["u"].reshape(N, 128, 128, 4)
    u[:, :, ::16] = 0
    for g in h[:4]: u[:, :, 16 * g] = (2.0 ** 30 * (1.0 - 0.1 * rng.random((N, 128, 4))) * rng.choice([-1.0, 1.0], (N, 1, 1))).astype(np.float32).astype(BF)
    for g in h[4:]: u[:, 16 * g + 8:16 * g + 16, 16 * g] = 2.0 ** -30
    u[e[2], :, ::16] = 0
    v = d["v"]
    v[e[:2]] = (2.0 ** 30 * rng.choice([-1.0, 1.0], (2, 128, 512))).astype(np.float32).astype(BF)
    a = rng.integers(0, 2, (2, N, 8, E)) * (E - 1)
    a[:, e[0]] = E - 1
    a[:, e[1]] = 0
    a[:, e[2]] = np.argsort(rng.random((2, 8, E)), axis=2)
    p, m = np.arange(C), rng.permutation(C)
    for g, k in enumerate(rng.permutation(8)):
        t = rng.permutation(E)
        if k == 0: t = np.concatenate([rng.permutation(C), C + rng.permutation(H)])
        elif H * (k - 1) < C: t = np.concatenate([C + rng.permutation(H), rng.permutation(C)])
        a[0, e[2], g, np.concatenate([p[np.roll(m, -H * (k - 1))], np.setdiff1d(np.arange(E), p)])] = t
        p = a[0, e[2], g, p]
    a[:, e[3]] = rng.integers(0, C, (2, 8, E))
    w = np.zeros((N, 128, 4, 128, 4), np.float32)
    i = np.flatnonzero(np.arange(128) % 16 < 8)
    k = rng.choice([-4.0, 4.0], (N, 1))
    for b in range(4): w[:, i, b, i, b] = k
    v = (np.where(v < 0, -1.0, 1.0) * np.where(rng.permutation(N) % 2, 2.0 ** -30, 2.0 ** 30)[:, None, None]).astype(np.float32).astype(BF)
    return {"x": x.astype(np.float32).reshape(N, 128, 4 * C).astype(BF), "u": u.reshape(N, 128, 512), "v": v, "lf": stored(a[0]), "rt": stored(a[1]), **weights(rng, w.astype(BF))}
def setup_inputs_spread(rng):
    d = numbers_of(rng)
    w = (layers(rng).astype(np.float32) * np.float32(0.125)).astype(BF)
    return {"x": big(wide(rng, N, 128, 4 * C, cols=4)), "u": d["u"], "v": d["v"], **lists(rng), **weights(rng, w)}
def check_inputs(d):
    b = []
    for k in ("x", "u", "v"):
        a = np.abs(d[k].astype(np.float32))
        if not (np.isfinite(a).all() and ((a == 0) | (a >= 2.0 ** -30) & (a <= 2.0 ** 30)).all()): b.append("a value of " + k)
    for k in ("lf", "rt"):
        if not ((d[k] >= 0) & (d[k] < E)).all(): b.append("an entry of " + k)
    none, least, most = [emit(mx_ref.quantize(np.full((128, 16), k, np.float32).astype(BF)))[1][0, 0] for k in (0.0, 2.0 ** -30, 2.0 ** 30)]
    size = 0.0
    for r in range(N):
        if ((d["wc"][r] == 0x7F) | (d["wc"][r] == 0xFF)).any(): b.append("wc: a code that is no number")
        s = mx_ref.live(d["ws"][r])
        if ((s != none) & ((s < least) | (s > most))).any(): b.append("ws: a scale out of range")
        full = ((d["wc"][r] & 0x7F) != 0).reshape(16, 8, 512, 4).any(axis=(1, 3))
        if (full & (s == none)).any(): b.append("wc: a code other than zero at the scale of zeros")
        with np.errstate(all="ignore"):
            size = np.maximum(size, np.max(np.sum(np.abs(decode(pk(d["wc"][r], d["ws"][r])).astype(np.float64)).reshape(128, 512, 4), axis=(0, 2))))
    with np.errstate(all="ignore"):
        if not np.max(np.abs(d["x"].astype(np.float64))) * (1.125 + 2.5 * size * 2.0 ** -5) ** 3 <= 2.0 ** 30: b.append("the sizes of x and W together")
    return b
def reference(x, u, v, lf, rt, wc, ws):
    qu = [mx_ref.quantize(u[r]) for r in range(N)]
    lay = [pk(wc[r], ws[r]) for r in range(N)]
    left = [gentries(lf[r]) for r in range(N)]
    right = [gentries(rt[r]) for r in range(N)]
    now = [x[r] for r in range(N)]
    took = np.zeros((N, 8, C), np.int64)
    for t in range(R):
        q = [mx_ref.quantize(now[r]) for r in range(N)]
        edge = [pick(q[r], np.arange(H)) for r in range(N)]
        own = [decode(q[r]) for r in range(N)]
        flux, back = [], []
        for r in range(N):
            e = (r + 1) % N
            s = np.abs(mx_ref.matmul(qu[r], join(q[r], edge[e]))[::16])
            l, k = np.arange(C), np.arange(C)
            for g in range(8):
                a, b = left[r][g, l], right[r][g, k]
                first = s[g, a] <= s[g, b]
                took[r, g] = np.where(first, a, b)
                l, k = np.where(first, a, l), np.where(first, k, b)
            window = np.concatenate([own[r], own[e][:, :4 * H]], axis=1).astype(BF)
            z = mx_ref.quantize(gcols(window, took[r]))
            h = mx_ref.quantize(tile([mx_ref.matmul(pick(lay[r], np.arange(128 * b, 128 * b + 128)), z) * np.float32(0.03125) for b in range(4)]))
            c = np.full((8, E), -1)
            for g in range(8):
                i, j = np.unique(took[r, g], return_index=True)
                c[g, i] = j
            w = gcols(decode(h).astype(BF), c)
            flux.append(w[:, :4 * C].astype(np.float32))
            back.append(decode(mx_ref.quantize(np.ascontiguousarray(w[:, 4 * C:]))))
        for r in range(N):
            n = own[r] - flux[r]
            n[:, :4 * H] = n[:, :4 * H] - back[(r - 1) % N]
            now[r] = n.astype(BF)
    y, on = np.zeros((N, 128, C), np.float32), np.zeros((N, 8, C), np.float32)
    oc, osc = np.zeros((N, 128, 4 * C), np.uint8), np.zeros((N, 16, C), np.uint8)
    for r in range(N):
        q = mx_ref.quantize(now[r])
        y[r] = mx_ref.matmul(mx_ref.quantize(v[r]), q)
        on[r] = took[r]
        oc[r], osc[r] = emit(q)
    return {"y": y, "on": on, "oc": oc, "osc": osc}

@@ -1,0 +1,426 @@
+from concourse.mybir import dt, AluOpType as ALU, ActivationFunctionType as AF
+
+ROUNDS = 3
+C, H, E = 320, 96, 416
+SCRATCH = {}
+
+
+def _declare(kind, names):
+    for w in names.split():
+        n, c = w.split(":")
+        SCRATCH[n] = ("psum" if n.startswith("ps") else "sbuf", [128, int(c)], kind)
+
+
+_declare("bfloat16", "xt:1280 ut:512 vin:512 eb:2048 vt:1664 mt:1280 tb:1280 tt:1296 ub:512")
+_declare("int32", "lri:52 pi:8 pa:8 pb:8 pq:8")
+_declare("uint16", "lru:52 l0:8 ll:8 cidx:20 nbu:16 na:32 nl:20 ml:80 adr:40 ul:104")
+_declare("float8_e4m3fn_x4", "qw:512 qu:128 qv:128 qe:512 qc:416 qm:320 qt:320 qr:224")
+_declare("uint8", "sw:512 su:128 sv:128 se:512 sc:416 sm:320 st:320 sr:224")
+_declare("float32", "idn:512 iw:416 tcol:416 dtq:416 tmp:416 tmp2:416 dsc:320 dia:416 jr:320 offc:64 c16:8 pf:8 ja:8 jb:8 jc:8")
+_declare("float32", "k0:8 k1:8 k2:8 k3:8 k4:8 k5:8 hs:8 q4:8 lr:832 dx:832 dn:832 bi:416 win:832 ts0:128 gt:128 tr:128")
+_declare("float32", "wv:64 nw:64 pt:8 nm:64 pn:64 nn:32 gf:256 tf:256 nlf:20 ss:416 sn:832 nr:320 eq:320 scn:320 tq:20")
+_declare("float32", "dup:20 dp:20 ad:20 inv0:432 inv1:432 dg0:416 dg1:416 dm:26 xf:384 ysb:320")
+_declare("float32", "ps0:512 ps1:512 ps2:512 ps3:512 ps4:512 ps5:512 ps6:512 ps7:512")
+SEMAPHORES = "cv cs ct cg lx0 lx1 llr lu lv lw stc rl nd ob bl rtl ba0 ba1 ba2 ra0 ra1 ra2".split()
+POS = {0: 0, 2: 1, 4: 2, 1: 3, 3: 4, 5: 5, 6: 6, 7: 7}
+
+
+def rank_program(g, core, T, topo):
+    rank = T.rank_of(core)
+    if rank is None:
+        return
+    nxt, prv = T.cores[(rank + 1) % 4], T.cores[(rank - 1) % 4]
+    eng = {"v": g.vector, "s": g.scalar, "t": g.tensor, "g": g, "y": g.sync}
+    csem = {"v": "cv", "s": "cs", "t": "ct", "g": "cg"}
+    cnt = {s: 0 for s in SEMAPHORES}
+    know = {q: {} for q in eng}
+    acc = {}
+    serial = [0]
+
+    def A(name, lo=0, hi=None, step=1, p=None, bits=None):
+        t = T[name]
+        hi = t.shape[1] if hi is None else hi
+        ps = slice(None) if p is None else slice(*p)
+        ap = t[ps, lo:hi] if step == 1 else t[ps, lo:hi:step]
+        if bits is not None:
+            ap = ap.bitcast(bits)
+        p0, p1 = (0, 128) if p is None else (p[0], p[1])
+        return {"ap": ap, "n": name, "lo": lo, "hi": hi, "st": step, "p0": p0, "p1": p1}
+
+    def meet(a, b):
+        if a["n"].startswith("ps"):
+            return True
+        if a["hi"] <= b["lo"] or b["hi"] <= a["lo"] or a["p1"] <= b["p0"] or b["p1"] <= a["p0"]:
+            return False
+        return not (a["st"] == b["st"] and a["st"] > 1 and (a["lo"] - b["lo"]) % a["st"])
+
+    def learn(q, rec, val):
+        k = know[q]
+        k[rec["sem"]] = max(k.get(rec["sem"], 0), val)
+        for s, c in rec["know"].items():
+            if k.get(s, 0) < c:
+                k[s] = c
+
+    def settle(q, reads, writes):
+        need = []
+        for kind, regs in ((0, reads), (1, writes)):
+            for r in regs:
+                for a in acc.get(r["n"], []):
+                    if not meet(r, a["reg"]):
+                        continue
+                    same = a["rec"]["q"] == q and not a["rec"]["late"]
+                    if kind == 0 and not a["w"] and (same or not r["n"].startswith("ps")):
+                        continue
+                    need.append(a["rec"])
+        need.sort(key=lambda rec: -rec["id"])
+        for rec in need:
+            val = cnt[rec["sem"]] if rec["late"] else rec["val"]
+            if know[q].get(rec["sem"], 0) >= val:
+                continue
+            eng[q].wait_ge(T.sem[rec["sem"]], val)
+            learn(q, rec, val)
+
+    def note(rec, reads, writes):
+        for w, regs in ((False, reads), (True, writes)):
+            for r in regs:
+                old = acc.get(r["n"], [])
+                if w and r["st"] == 1:
+                    old = [a for a in old if not (a["reg"]["lo"] >= r["lo"] and a["reg"]["hi"] <= r["hi"] and a["reg"]["p0"] >= r["p0"] and a["reg"]["p1"] <= r["p1"])]
+                old.append({"reg": r, "rec": rec, "w": w})
+                acc[r["n"]] = old
+
+    def op(q, fn, writes, reads, sem=None, inc=1, self_inc=False):
+        settle(q, reads, writes)
+        s = sem or csem[q]
+        ins = fn()
+        if not self_inc:
+            ins.then_inc(T.sem[s], inc)
+        cnt[s] += inc
+        serial[0] += 1
+        note({"q": q, "sem": s, "val": cnt[s], "late": sem is not None, "know": dict(know[q]), "id": serial[0]}, reads, writes)
+
+    def arrive(sem, n, writes):
+        cnt[sem] += n
+        serial[0] += 1
+        note({"q": "far", "sem": sem, "val": cnt[sem], "late": True, "know": {}, "id": serial[0]}, [], writes)
+
+    def copy(out, i):
+        op("v", lambda: g.vector.tensor_copy(out["ap"], i["ap"]), [out], [i])
+
+    def pick(out, i, off):
+        op("v", lambda: g.vector.tensor_copy(out["ap"], i["ap"].indirect(off["ap"])), [out], [i, off])
+
+    def put(out, off, i):
+        op("v", lambda: g.vector.tensor_copy(out["ap"].indirect(off["ap"]), i["ap"]), [out], [off, i])
+
+    def tt(out, a, b, o, off=None):
+        ia = a["ap"] if off is None else a["ap"].indirect(off["ap"])
+        op("v", lambda: g.vector.tensor_tensor(out["ap"], ia, b["ap"], o), [out], [a, b] + ([off] if off else []))
+
+    def ts(out, a, s1, o1, s2=None, o2=None, off=None):
+        ia = a["ap"] if off is None else a["ap"].indirect(off["ap"])
+        rd = [a] + [s for s in (s1, s2, off) if isinstance(s, dict)]
+        v1 = s1["ap"] if isinstance(s1, dict) else s1
+        v2 = s2["ap"] if isinstance(s2, dict) else s2
+        if o2 is None:
+            op("v", lambda: g.vector.tensor_scalar(out["ap"], ia, v1, None, o1), [out], rd)
+        else:
+            op("v", lambda: g.vector.tensor_scalar(out["ap"], ia, v1, v2, o1, o2), [out], rd)
+
+    def scan(out, d0, d1, o0, o1):
+        op("v", lambda: g.vector.tensor_tensor_scan(out["ap"], d0["ap"], d1["ap"], 0.0, o0, o1), [out], [d0, d1])
+
+    def turn(out, i):
+        op("v", lambda: g.vector.transpose(out["ap"], i["ap"]), [out], [i])
+
+    def fill(out, c):
+        op("v", lambda: g.vector.memset(out["ap"], c), [out], [])
+
+    def act(out, i, func=AF.Copy, scale=1.0, off=None):
+        ia = i["ap"] if off is None else i["ap"].indirect(off["ap"])
+        op("s", lambda: g.scalar.activation(out["ap"], ia, func, scale=scale), [out], [i] + ([off] if off else []))
+
+    def quant(k, lo, hi, src):
+        o, s = A("q" + k, lo, hi), A("s" + k, lo, hi)
+        op("v", lambda: g.vector.quantize_mx(o["ap"], s["ap"], src["ap"]), [o, s], [src])
+
+    def mm(bank, w, wlo, x, lo, hi):
+        o = A("ps%d" % bank, 0, hi - lo)
+        a, b, c, d = A("q" + w, wlo, wlo + 128), A("s" + w, wlo, wlo + 128), A("q" + x, lo, hi), A("s" + x, lo, hi)
+        op("t", lambda: g.tensor.matmul_mx(o["ap"], a["ap"], b["ap"], c["ap"], d["ap"], True, True), [o], [a, b, c, d])
+
+    def P(bank, lo, hi):
+        return A("ps%d" % bank, lo, hi)
+
+    def dma(q, sem, out, i):
+        w, rd = [[a] if isinstance(a, dict) else [] for a in (out, i)]
+        oa, ia = [a["ap"] if isinstance(a, dict) else a for a in (out, i)]
+        op(q, lambda: eng[q].dma_start(oa, ia), w, rd, sem=sem, inc=16)
+
+    def iota(o, pattern, cm):
+        op("g", lambda: g.iota(o["ap"], pattern, 0, cm, allow_small_or_imprecise_dtypes=True), [o], [])
+
+    def send(dst, k, a, b, c, rsem, lsem):
+        rid, pid = topo.addr(dst)[:2]
+        mask, n = topo.mask(core, dst), len(topo.engines(core, dst))
+        for name, bits in (("q" + k, dt.uint8), ("s" + k, None)):
+            i, o = A(name, a, b, bits=bits), A(name, c, c + b - a, bits=bits)
+            op("g", lambda: g.remote_dma(o["ap"], i["ap"], T.sem[rsem], T.sem[lsem], pid, rid, mask), [], [i], sem=lsem, inc=n, self_inc=True)
+
+    def unpack(banks, lo, hi, who, skip=0):
+        for b in range(4):
+            mm(banks[b], "e", 128 * b, "c", lo, hi)
+        for b in range(4):
+            o, i = A("vt", 4 * (lo + skip) + b, 4 * hi, 4), P(banks[b], skip, hi - lo)
+            copy(o, i) if who[b] == "v" else act(o, i)
+
+    def score(bank, lo, hi, skip=0):
+        mm(bank, "u", 0, "c", lo, hi)
+        act(A("ss", lo + skip, hi), P(bank, skip, hi - lo), AF.Abs)
+
+    def border_out(r):
+        send(prv, "c", 0, H, C, "ba%d" % r, "bl")
+
+    dma("y", "lx0", A("xt", 0, 512), T.x[:, 0:512])
+    dma("s", "llr", A("lri", 0, 26), T.lf[:, :])
+    dma("y", "lx1", A("xt", 512, 1280), T.x[:, 512:1280])
+    dma("s", "llr", A("lri", 26, 52), T.rt[:, :])
+    dma("y", "lu", A("ut"), T.u[:, :])
+    dma("s", "lw", A("qw", bits=dt.uint8), T.wc[:, :])
+    dma("s", "lw", A("sw"), T.ws[:, :])
+    dma("y", "lv", A("vin"), T.v[:, :])
+    pi = A("pi")
+    op("g", lambda: g.iota(pi["ap"], [[0, 8]], 0, 1), [pi], [])
+    iota(A("c16"), [[416, 2], [256, 2], [16, 2]], 0)
+    iota(A("iw"), [[1, 416]], 0)
+    iota(A("idn"), [[1, 512]], -4)
+
+    copy(A("pf", 0, 1), A("pi", 0, 1))
+    ts(A("k0", 0, 1), A("pf", 0, 1), 0.0, ALU.is_equal)
+    ts(A("k1", 0, 1), A("pf", 0, 1), 112.0, ALU.is_equal)
+    ts(A("k2", 0, 1), A("k0", 0, 1), -1.0, ALU.mult, 1.0, ALU.add)
+    ts(A("k3", 0, 1), A("k0", 0, 1), 2.0, ALU.mult, -1.0, ALU.add)
+    tt(A("k4", 0, 1), A("k3", 0, 1), A("k1", 0, 1), ALU.add)
+    ts(A("k5", 0, 1), A("k0", 0, 1), 416.0, ALU.mult)
+    for lo in (0, 4):
+        ts(A("pa", lo, lo + 2), A("pi", lo, lo + 2), 7, ALU.bitwise_and)
+        ts(A("pb", lo, lo + 2), A("pi", lo, lo + 2), 3, ALU.logical_shift_right)
+        ts(A("pa", lo + 2, lo + 4), A("pi", lo + 2, lo + 4), 1, ALU.bitwise_and)
+        ts(A("pb", lo + 2, lo + 4), A("pi", lo + 2, lo + 4), 1, ALU.logical_shift_right)
+    ts(A("ja"), A("pa"), 32.0, ALU.mult)
+    tt(A("jb"), A("ja"), A("pb"), ALU.add)
+    tt(A("jc"), A("jb"), A("c16"), ALU.add)
+    copy(A("l0"), A("jc"))
+
+    quant("c", 0, 128, A("xt", 0, 512))
+    border_out(0)
+    iota(A("offc"), [[0, 8], [416, 2], [0, 4]], 0)
+    iota(A("tcol"), [[0, 26], [1, 16]], 0)
+    copy(A("lru"), A("lri"))
+    quant("c", 128, 320, A("xt", 512, 1280))
+    quant("u", 0, 128, A("ut"))
+    score(0, 0, 128)
+    score(6, 128, 320)
+    pick(A("lr"), A("iw"), A("lru"))
+    ts(A("bi"), A("iw"), A("k4", 0, 1), ALU.mult)
+    ts(A("dx", 0, 416), A("lr", 0, 416), A("k2", 0, 1), ALU.mult)
+    ts(A("dx", 416, 832), A("lr", 416, 832), A("k2", 0, 1), ALU.mult, A("k5", 0, 1), ALU.add)
+    tt(A("dn", 0, 416), A("dx", 0, 416), A("bi"), ALU.add)
+    tt(A("dn", 416, 832), A("dx", 416, 832), A("bi"), ALU.add)
+    for h in range(8):
+        for k in range(2):
+            dma("y", "stc", A("win", p=(16 * h + 8 * k, 16 * h + 8 * k + 8)), A("dn", p=(1 - k, 128, 16)))
+    for b in range(4):
+        ts(A("eb", 512 * b, 512 * b + 512), A("idn"), float(b), ALU.is_equal)
+    quant("e", 0, 512, A("eb"))
+    unpack((2, 3, 4, 5), 0, 128, "ssss")
+    unpack((7, 1, 2, 3), 128, 320, "ssss")
+    pick(A("gt"), A("win"), A("l0"))
+    turn(A("ts0"), A("gt"))
+
+    def constants():
+        copy(A("cidx"), A("iw", 0, 20))
+        ts(A("pq", 0, 1), A("pi", 0, 1), 15, ALU.bitwise_and)
+        copy(A("pf", 1, 2), A("pq", 0, 1))
+        ts(A("hs", 0, 1), A("pf", 1, 2), 15.0, ALU.is_lt, 2000.0, ALU.mult)
+        ts(A("q4", 0, 1), A("pf", 1, 2), 416.0, ALU.add)
+        ts(A("dtq"), A("tcol"), A("pf", 1, 2), ALU.subtract)
+        ts(A("tmp", 0, 320), A("dtq", 0, 320), 0.0, ALU.is_equal, 63.0, ALU.mult)
+        ts(A("tmp2", 0, 320), A("tcol", 0, 320), 0.0, ALU.is_gt)
+        ts(A("dsc"), A("tmp", 0, 320), 1.0, ALU.add)
+        tt(A("dsc"), A("dsc"), A("tmp2", 0, 320), ALU.mult)
+        ts(A("tmp"), A("dtq"), 0.0, ALU.is_equal, -4000.0, ALU.mult)
+        ts(A("tmp2"), A("dtq"), 1.0, ALU.is_equal, 2000.0, ALU.mult)
+        tt(A("dia"), A("tmp"), A("tmp2"), ALU.add)
+        ts(A("jr"), A("iw", 0, 320), 4.0, ALU.mult)
+        fill(A("tt", 1280, 1296), 0.0)
+        fill(A("ub", 384, 512), 0.0)
+        quant("v", 0, 128, A("vin"))
+
+    def to_list(gi):
+        c, p = 4 * POS[gi], (16 * gi, 16 * gi + 16)
+        dma("y", "nd", A("nl", 0, 16, p=p), A("na", c, c + 2))
+        dma("y", "nd", A("nl", 16, 20, p=p), A("na", c + 2, c + 4, p=(0, 32)))
+
+    def batch():
+        yield lambda: tt(A("nm", 0, 48), A("nw", 0, 48), A("offc", 0, 48), ALU.subtract)
+        yield lambda: tt(A("pn", 0, 48), A("nm", 0, 48), A("wv", 0, 48), ALU.mult)
+        for c in range(4):
+            yield lambda c=c: tt(A("nn", c, 24, 4), A("pn", c, 48, 8), A("pn", c + 4, 48, 8), ALU.add)
+
+        def out():
+            copy(A("nbu", 0, 12), A("nn", 0, 12))
+            act(A("gf", 0, 192), A("win"), off=A("nbu", 0, 12))
+        yield out
+
+        def out2():
+            copy(A("na", 12, 24), A("nn", 12, 24))
+            for gi in (1, 3, 5):
+                to_list(gi)
+        yield out2
+        yield lambda: turn(A("tf", 0, 192), A("gf", 0, 192))
+
+        def out3():
+            copy(A("na", 0, 12), A("tf", 8, 192, 16))
+            for gi in (0, 2, 4):
+                to_list(gi)
+        yield out3
+
+    def growth():
+        todo = []
+
+        def gap():
+            if todo:
+                todo.pop(0)()
+        for s in range(8):
+            a = 8 * POS[s]
+            pick(A("gt"), A("win"), A("l0") if s == 0 else A("ll"))
+            if s < 7:
+                gap()
+                turn(A("tr"), A("gt"))
+                gap()
+            else:
+                tt(A("nm", 48, 56), A("nw", 48, 56), A("offc", 48, 56), ALU.subtract)
+                turn(A("tr"), A("gt"))
+                tt(A("pn", 48, 56), A("nm", 48, 56), A("wv", 48, 56), ALU.mult)
+            tt(A("wv", a, a + 4), A("tr", s, 64, 16), A("tr", 64 + s, 128, 16), ALU.is_le)
+            tt(A("wv", a + 4, a + 8), A("tr", s, 64, 16), A("tr", 64 + s, 128, 16), ALU.is_gt)
+            if s == 7:
+                tt(A("nn", 24, 28), A("pn", 48, 52), A("pn", 52, 56), ALU.add)
+                tt(A("pn", 56, 64), A("wv", 56, 64), A("tr", 15, 128, 16), ALU.mult)
+                copy(A("nbu", 12, 16), A("nn", 24, 28))
+                act(A("gf", 192, 256), A("win"), off=A("nbu", 12, 16))
+                tt(A("nn", 28, 32), A("pn", 56, 60), A("pn", 60, 64), ALU.add)
+                gap()
+                copy(A("na", 28, 32), A("nn", 28, 32))
+                to_list(7)
+                turn(A("tf", 192, 256), A("gf", 192, 256))
+                gap()
+                copy(A("na", 24, 28), A("tf", 200, 256, 16))
+                to_list(6)
+                while todo:
+                    gap()
+                break
+            gap()
+            dif = A("ts0", 0, 128, 16) if s == 0 else A("tr", 8 + s, 128, 16)
+            base = A("ts0", 8, 128, 16) if s == 0 else A("tr", 8, 128, 16)
+            tt(A("pt"), A("wv", a, a + 8), dif, ALU.mult)
+            gap()
+            tt(A("nw", a, a + 8), A("pt"), base, ALU.add)
+            gap()
+            copy(A("ll"), A("nw", a, a + 8))
+            if s == 5:
+                todo.extend(batch())
+
+    n_in_b = 2 * len(topo.engines(nxt, core))
+    n_in_r = 2 * len(topo.engines(prv, core))
+    for r in range(ROUNDS):
+        last = r == ROUNDS - 1
+        arrive("ba%d" % r, n_in_b, [A("qc", C, E), A("sc", C, E)])
+        score(1, 288, 416, 32)
+        pick(A("sn", 0, 416), A("ss"), A("lru", 0, 26))
+        act(A("sn", 416, 832), A("ss"), off=A("lru", 26, 52))
+        for h in range(8):
+            dma("y" if h < 4 else "s", "rl", A("win", p=(16 * h, 16 * h + 8)), A("sn", p=(0, 128, 16)))
+        unpack((2, 3, 4, 5), 288, 416, "vvss", 32)
+        fill(A("inv0"), 1280.0)
+        fill(A("inv1"), 1280.0)
+        if r == 0:
+            constants()
+        growth()
+        for t in (2, 3, 0, 1):
+            ts(A("ml", 20 * t, 20 * t + 20), A("nl"), 4.0, ALU.mult, float(t), ALU.add)
+        for t in (2, 3):
+            act(A("mt", t, 1280, 4), A("vt"), off=A("ml", 20 * t, 20 * t + 20))
+        for t in (0, 1):
+            pick(A("mt", t, 1280, 4), A("vt"), A("ml", 20 * t, 20 * t + 20))
+        copy(A("nlf"), A("nl"))
+        quant("m", 0, 320, A("mt"))
+        hb = (0, 1, 6, 7)
+        for b in range(4):
+            mm(hb[b], "w", 128 * b, "m", 0, 320)
+        for b in range(4):
+            act(A("tb", b, 1280, 4), P(hb[b], 0, 320), scale=0.03125)
+        pick(A("nr"), A("iw"), A("nl"))
+        ts(A("tq"), A("nlf"), -1.0, ALU.mult, A("q4", 0, 1), ALU.add)
+        tt(A("eq"), A("nlf"), A("nr"), ALU.is_equal, off=A("cidx"))
+        if last:
+            dma("y", "ob", T.on[:, :], A("nr", p=(0, 128, 16)))
+        scan(A("scn"), A("dsc"), A("eq"), ALU.mult, ALU.add)
+        ts(A("dup"), A("scn", 15, 320, 16), 32.0, ALU.is_ge)
+        tt(A("dp"), A("dup"), A("tq"), ALU.mult)
+        tt(A("ad"), A("nlf"), A("dp"), ALU.add)
+        copy(A("adr", 0, 40, 2), A("ad"))
+        quant("t", 0, 320, A("tb"))
+        for b in range(4):
+            mm(2 + b, "e", 128 * b, "t", 0, 320)
+        for b in range(4):
+            act(A("tt", b, 1280, 4), P(2 + b, 0, 320), scale=-1.0)
+        for c in range(9, -1, -1):
+            for k in (1, 0):
+                d = 10 * k + c
+                put(A("inv%d" % k), A("adr", 2 * d, 2 * d + 1), A("jr", 16 * d, 16 * d + 16))
+        for k in (1, 0):
+            scan(A("dg%d" % k), A("dia"), A("inv%d" % k, 0, 416), ALU.add, ALU.max)
+        tt(A("dm"), A("dg0", 15, 416, 16), A("dg1", 15, 416, 16), ALU.min)
+        for t in (2, 3, 0, 1):
+            ts(A("ul", 26 * t, 26 * t + 26), A("dm"), A("hs", 0, 1), ALU.subtract, float(t), ALU.add)
+        for t in (2, 3):
+            act(A("ub", t, 384, 4), A("tt"), scale=-1.0, off=A("ul", 26 * t + 20, 26 * t + 26))
+        for t in (0, 1):
+            ts(A("ub", t, 384, 4), A("tt"), -1.0, ALU.mult, off=A("ul", 26 * t + 20, 26 * t + 26))
+        quant("r", 0, 128, A("ub"))
+        send(nxt, "r", 0, H, 128, "ra%d" % r, "rtl")
+        for t in range(4):
+            tt(A("xt", 384 + t, 1280, 4), A("tt"), A("vt", 384 + t, 1280, 4), ALU.add, off=A("ul", 26 * t + 6, 26 * t + 20))
+        quant("c", 128, 320, A("xt", 512, 1280))
+        for t in range(4):
+            tt(A("xf", t, 384, 4), A("tt"), A("vt", t, 384, 4), ALU.add, off=A("ul", 26 * t, 26 * t + 6))
+        if last:
+            mm(6, "v", 0, "c", 128, 320)
+            act(A("ysb", 128, 320), P(6, 0, 192))
+            dma("y", "ob", T.y[:, 128:320], A("ysb", 128, 320))
+        else:
+            score(6, 128, 320)
+            unpack((2, 3, 4, 5), 128, 320, "ssss")
+        arrive("ra%d" % r, n_in_r, [A("qr", 128, 224), A("sr", 128, 224)])
+        bb = (0, 1, 7, 6)
+        for b in range(4):
+            mm(bb[b], "e", 128 * b, "r", 96, 224)
+        for b in range(4):
+            tt(A("xt", b, 384, 4), A("xf", b, 384, 4), P(bb[b], 32, 128), ALU.subtract)
+        quant("c", 0, 128, A("xt", 0, 512))
+        if last:
+            mm(0, "v", 0, "c", 0, 128)
+            act(A("ysb", 0, 128), P(0, 0, 128))
+            dma("y", "ob", T.oc[:, :], A("qc", 0, 320, bits=dt.uint8))
+            for k in range(4):
+                dma("y" if k % 2 else "s", "ob", T.osc[4 * k:4 * k + 4, 0:320], A("sc", 0, 320, p=(32 * k, 32 * k + 4)))
+            dma("s", "ob", T.y[:, 0:128], A("ysb", 0, 128))
+        else:
+            border_out(r + 1)
+            score(0, 0, 128)
+            unpack((2, 3, 4, 5), 0, 128, "vvss")
+    for s in SEMAPHORES:
+        if know["g"].get(s, 0) < cnt[s]:
+            g.wait_ge(T.sem[s], cnt[s])

@@ -11,18 +11,18 @@ def _declare(kind, names):
         SCRATCH[n] = ("psum" if n.startswith("ps") else "sbuf", [128, int(c)], kind)
 
 
-_declare("bfloat16", "xt:1280 ut:512 vin:512 eb:2048 vt:1664 mt:1280 tb:1280 tt:1296 ub:512")
+_declare("bfloat16", "xt:1280 ut:512 vin:512 eb:516 vt:1664 mt:1280 tb:1280 tt:1296 ub:512")
 _declare("int32", "lri:52 pi:8 pa:8 pb:8 pq:8")
-_declare("uint16", "lru:52 l0:8 ll:8 cidx:20 nbu:16 na:32 nl:20 ml:80 adr:40 ul:104")
+_declare("uint16", "lru:52 l0:8 ll:8 cidx:20 nbu:32 na:32 nl:20 ml:80 qrep:26 adr:40 ul:80 ulb:24")
 _declare("float8_e4m3fn_x4", "qw:512 qu:128 qv:128 qe:512 qc:416 qm:320 qt:320 qr:224")
 _declare("uint8", "sw:512 su:128 sv:128 se:512 sc:416 sm:320 st:320 sr:224")
-_declare("float32", "idn:512 iw:416 tcol:416 dtq:416 tmp:416 tmp2:416 dsc:320 dia:416 jr:320 offc:64 c16:8 pf:8 ja:8 jb:8 jc:8")
-_declare("float32", "k0:8 k1:8 k2:8 k3:8 k4:8 k5:8 hs:8 q4:8 lr:832 dx:832 dn:832 bi:416 win:832 ts0:128 gt:128 tr:128")
-_declare("float32", "wv:64 nw:64 pt:8 nm:64 pn:64 nn:32 gf:256 tf:256 nlf:20 ss:416 sn:832 nr:320 eq:320 scn:320 tq:20")
+_declare("float32", "idn:516 iw:432 cs:96 dsc:320 dia:416 jr:320 offc:64 c16:8 pf:8 ja:8 jb:8 jc:8")
+_declare("float32", "k0:8 k1:8 k2:8 k3:8 k4:8 k5:8 hs:8 q4:8 dn:832 aiw:416 bi:832 win:832 ts0:128 gt:128 tr:128")
+_declare("float32", "wv:64 nw:64 pt:8 nm:64 pn:64 nn:32 gf:512 tf:512 nlf:20 ss:416 sn:832 nr:320 eq:320 scn:320 tq:20")
 _declare("float32", "dup:20 dp:20 ad:20 inv0:432 inv1:432 dg0:416 dg1:416 dm:26 xf:384 ysb:320")
 _declare("float32", "ps0:512 ps1:512 ps2:512 ps3:512 ps4:512 ps5:512 ps6:512 ps7:512")
 SEMAPHORES = "cv cs ct cg lx0 lx1 llr lu lv lw stc rl nd ob bl rtl ba0 ba1 ba2 ra0 ra1 ra2".split()
-POS = {0: 0, 2: 1, 4: 2, 1: 3, 3: 4, 5: 5, 6: 6, 7: 7}
+POS = {0: 0, 2: 1, 1: 2, 3: 3, 4: 4, 5: 5, 6: 6, 7: 7}
 
 
 def rank_program(g, core, T, topo):
@@ -74,9 +74,9 @@ def rank_program(g, core, T, topo):
                     need.append(a["rec"])
         need.sort(key=lambda rec: -rec["id"])
         for rec in need:
-            val = cnt[rec["sem"]] if rec["late"] else rec["val"]
-            if know[q].get(rec["sem"], 0) >= val:
+            if know[q].get(rec["sem"], 0) >= rec["val"]:
                 continue
+            val = cnt[rec["sem"]] if rec["late"] else rec["val"]
             eng[q].wait_ge(T.sem[rec["sem"]], val)
             learn(q, rec, val)
 
@@ -136,9 +136,11 @@ def rank_program(g, core, T, topo):
     def fill(out, c):
         op("v", lambda: g.vector.memset(out["ap"], c), [out], [])
 
-    def act(out, i, func=AF.Copy, scale=1.0, off=None):
+    def act(out, i, func=AF.Copy, scale=1.0, off=None, bias=0.0):
         ia = i["ap"] if off is None else i["ap"].indirect(off["ap"])
-        op("s", lambda: g.scalar.activation(out["ap"], ia, func, scale=scale), [out], [i] + ([off] if off else []))
+        sv, bv = [s["ap"] if isinstance(s, dict) else s for s in (scale, bias)]
+        rd = [i] + [s for s in (off, scale, bias) if isinstance(s, dict)]
+        op("s", lambda: g.scalar.activation(out["ap"], ia, func, scale=sv, bias=bv), [out], rd)
 
     def quant(k, lo, hi, src):
         o, s = A("q" + k, lo, hi), A("s" + k, lo, hi)
@@ -192,97 +194,99 @@ def rank_program(g, core, T, topo):
     pi = A("pi")
     op("g", lambda: g.iota(pi["ap"], [[0, 8]], 0, 1), [pi], [])
     iota(A("c16"), [[416, 2], [256, 2], [16, 2]], 0)
-    iota(A("iw"), [[1, 416]], 0)
-    iota(A("idn"), [[1, 512]], -4)
+    iota(A("iw"), [[1, 432]], 0)
+    iota(A("idn"), [[1, 516]], -4)
+    iota(A("offc"), [[0, 8], [416, 2], [0, 4]], 0)
 
+    z, q = A("k0", 0, 1), A("pf", 1, 2)
     copy(A("pf", 0, 1), A("pi", 0, 1))
-    ts(A("k0", 0, 1), A("pf", 0, 1), 0.0, ALU.is_equal)
+    ts(A("pq", 0, 1), A("pi", 0, 1), 15, ALU.bitwise_and)
+    ts(z, A("pf", 0, 1), 0.0, ALU.is_equal)
     ts(A("k1", 0, 1), A("pf", 0, 1), 112.0, ALU.is_equal)
-    ts(A("k2", 0, 1), A("k0", 0, 1), -1.0, ALU.mult, 1.0, ALU.add)
-    ts(A("k3", 0, 1), A("k0", 0, 1), 2.0, ALU.mult, -1.0, ALU.add)
+    copy(q, A("pq", 0, 1))
+    ts(A("k2", 0, 1), z, -1.0, ALU.mult, 1.0, ALU.add)
+    ts(A("k3", 0, 1), z, 2.0, ALU.mult, -1.0, ALU.add)
+    ts(A("k5", 0, 1), z, 416.0, ALU.mult)
     tt(A("k4", 0, 1), A("k3", 0, 1), A("k1", 0, 1), ALU.add)
-    ts(A("k5", 0, 1), A("k0", 0, 1), 416.0, ALU.mult)
     for lo in (0, 4):
         ts(A("pa", lo, lo + 2), A("pi", lo, lo + 2), 7, ALU.bitwise_and)
         ts(A("pb", lo, lo + 2), A("pi", lo, lo + 2), 3, ALU.logical_shift_right)
         ts(A("pa", lo + 2, lo + 4), A("pi", lo + 2, lo + 4), 1, ALU.bitwise_and)
         ts(A("pb", lo + 2, lo + 4), A("pi", lo + 2, lo + 4), 1, ALU.logical_shift_right)
+    ts(A("hs", 0, 1), q, 15.0, ALU.is_lt, 2000.0, ALU.mult)
     ts(A("ja"), A("pa"), 32.0, ALU.mult)
+    ts(A("q4", 0, 1), q, 416.0, ALU.add)
     tt(A("jb"), A("ja"), A("pb"), ALU.add)
+    fill(A("tt", 1280, 1296), 0.0)
     tt(A("jc"), A("jb"), A("c16"), ALU.add)
+    fill(A("ub", 384, 512), 0.0)
     copy(A("l0"), A("jc"))
+    t16, d16 = A("iw", 0, 16), A("cs", 32, 48)
+    ts(d16, t16, q, ALU.subtract)
+    ts(A("cs", 80, 96), t16, 0.0, ALU.is_gt)
+    ts(A("qrep"), A("iw", 0, 26), 0.0, ALU.mult, q, ALU.add)
+    ts(A("cs", 48, 64), d16, 0.0, ALU.is_equal, -4000.0, ALU.mult)
+    ts(A("cs", 64, 80), d16, 1.0, ALU.is_equal, 2000.0, ALU.mult)
+    ts(d16, d16, 0.0, ALU.is_equal, 63.0, ALU.mult)
+    tt(A("cs", 16, 32), A("cs", 48, 64), A("cs", 64, 80), ALU.add)
+    ts(d16, d16, 1.0, ALU.add)
+    copy(A("cidx"), A("iw", 0, 20))
+    tt(A("cs", 0, 16), d16, A("cs", 80, 96), ALU.mult)
+    ts(A("eb"), A("idn"), 3.0, ALU.is_equal)
+    w16 = A("iw", 0, E)
+    act(A("aiw"), w16, scale=A("k2", 0, 1))
+    act(A("bi", 0, 416), w16, scale=A("k4", 0, 1))
+    act(A("bi", 416, 832), w16, AF.Identity, scale=A("k4", 0, 1), bias=A("k5", 0, 1))
+    act(A("jr"), A("iw", 0, 320), scale=4.0)
+    act(A("dsc"), A("cs", 0, 16), off=A("qrep", 0, 20))
+    act(A("dia"), A("cs", 16, 32), off=A("qrep", 0, 26))
 
     quant("c", 0, 128, A("xt", 0, 512))
     border_out(0)
-    iota(A("offc"), [[0, 8], [416, 2], [0, 4]], 0)
-    iota(A("tcol"), [[0, 26], [1, 16]], 0)
     copy(A("lru"), A("lri"))
-    quant("c", 128, 320, A("xt", 512, 1280))
     quant("u", 0, 128, A("ut"))
     score(0, 0, 128)
-    score(6, 128, 320)
-    pick(A("lr"), A("iw"), A("lru"))
-    ts(A("bi"), A("iw"), A("k4", 0, 1), ALU.mult)
-    ts(A("dx", 0, 416), A("lr", 0, 416), A("k2", 0, 1), ALU.mult)
-    ts(A("dx", 416, 832), A("lr", 416, 832), A("k2", 0, 1), ALU.mult, A("k5", 0, 1), ALU.add)
-    tt(A("dn", 0, 416), A("dx", 0, 416), A("bi"), ALU.add)
-    tt(A("dn", 416, 832), A("dx", 416, 832), A("bi"), ALU.add)
+    tt(A("dn"), A("aiw"), A("bi"), ALU.add, off=A("lru"))
     for h in range(8):
         for k in range(2):
-            dma("y", "stc", A("win", p=(16 * h + 8 * k, 16 * h + 8 * k + 8)), A("dn", p=(1 - k, 128, 16)))
+            dma("y" if h < 5 else "s", "stc", A("win", p=(16 * h + 8 * k, 16 * h + 8 * k + 8)), A("dn", p=(1 - k, 128, 16)))
+    quant("c", 128, 320, A("xt", 512, 1280))
+    score(6, 128, 320)
     for b in range(4):
-        ts(A("eb", 512 * b, 512 * b + 512), A("idn"), float(b), ALU.is_equal)
-    quant("e", 0, 512, A("eb"))
-    unpack((2, 3, 4, 5), 0, 128, "ssss")
+        quant("e", 128 * b, 128 * b + 128, A("eb", 3 - b, 515 - b))
+    unpack((2, 3, 4, 5), 0, 128, "vvss")
     unpack((7, 1, 2, 3), 128, 320, "ssss")
     pick(A("gt"), A("win"), A("l0"))
     turn(A("ts0"), A("gt"))
-
-    def constants():
-        copy(A("cidx"), A("iw", 0, 20))
-        ts(A("pq", 0, 1), A("pi", 0, 1), 15, ALU.bitwise_and)
-        copy(A("pf", 1, 2), A("pq", 0, 1))
-        ts(A("hs", 0, 1), A("pf", 1, 2), 15.0, ALU.is_lt, 2000.0, ALU.mult)
-        ts(A("q4", 0, 1), A("pf", 1, 2), 416.0, ALU.add)
-        ts(A("dtq"), A("tcol"), A("pf", 1, 2), ALU.subtract)
-        ts(A("tmp", 0, 320), A("dtq", 0, 320), 0.0, ALU.is_equal, 63.0, ALU.mult)
-        ts(A("tmp2", 0, 320), A("tcol", 0, 320), 0.0, ALU.is_gt)
-        ts(A("dsc"), A("tmp", 0, 320), 1.0, ALU.add)
-        tt(A("dsc"), A("dsc"), A("tmp2", 0, 320), ALU.mult)
-        ts(A("tmp"), A("dtq"), 0.0, ALU.is_equal, -4000.0, ALU.mult)
-        ts(A("tmp2"), A("dtq"), 1.0, ALU.is_equal, 2000.0, ALU.mult)
-        tt(A("dia"), A("tmp"), A("tmp2"), ALU.add)
-        ts(A("jr"), A("iw", 0, 320), 4.0, ALU.mult)
-        fill(A("tt", 1280, 1296), 0.0)
-        fill(A("ub", 384, 512), 0.0)
-        quant("v", 0, 128, A("vin"))
 
     def to_list(gi):
         c, p = 4 * POS[gi], (16 * gi, 16 * gi + 16)
         dma("y", "nd", A("nl", 0, 16, p=p), A("na", c, c + 2))
         dma("y", "nd", A("nl", 16, 20, p=p), A("na", c + 2, c + 4, p=(0, 32)))
 
-    def batch():
-        yield lambda: tt(A("nm", 0, 48), A("nw", 0, 48), A("offc", 0, 48), ALU.subtract)
-        yield lambda: tt(A("pn", 0, 48), A("nm", 0, 48), A("wv", 0, 48), ALU.mult)
-        for c in range(4):
-            yield lambda c=c: tt(A("nn", c, 24, 4), A("pn", c, 48, 8), A("pn", c + 4, 48, 8), ALU.add)
+    def batch(even, odd):
+        lo, k = POS[even[0]], len(even)
+        mid, hi = lo + k, lo + 2 * k
+        yield lambda: tt(A("nm", 8 * lo, 8 * hi), A("nw", 8 * lo, 8 * hi), A("offc", 8 * lo, 8 * hi), ALU.subtract)
+        yield lambda: tt(A("pn", 8 * lo, 8 * hi), A("nm", 8 * lo, 8 * hi), A("wv", 8 * lo, 8 * hi), ALU.mult)
+        for s in range(lo, hi):
+            yield lambda s=s: tt(A("nn", 4 * s, 4 * s + 4), A("pn", 8 * s, 8 * s + 4), A("pn", 8 * s + 4, 8 * s + 8), ALU.add)
 
         def out():
-            copy(A("nbu", 0, 12), A("nn", 0, 12))
-            act(A("gf", 0, 192), A("win"), off=A("nbu", 0, 12))
+            copy(A("nbu", 4 * lo, 4 * mid), A("nn", 4 * lo, 4 * mid))
+            act(A("gf", 64 * lo, 64 * mid), A("win"), off=A("nbu", 4 * lo, 4 * mid))
         yield out
 
         def out2():
-            copy(A("na", 12, 24), A("nn", 12, 24))
-            for gi in (1, 3, 5):
+            copy(A("na", 4 * mid, 4 * hi), A("nn", 4 * mid, 4 * hi))
+            for gi in odd:
                 to_list(gi)
         yield out2
-        yield lambda: turn(A("tf", 0, 192), A("gf", 0, 192))
+        yield lambda: turn(A("tf", 64 * lo, 64 * mid), A("gf", 64 * lo, 64 * mid))
 
         def out3():
-            copy(A("na", 0, 12), A("tf", 8, 192, 16))
-            for gi in (0, 2, 4):
+            copy(A("na", 4 * lo, 4 * mid), A("tf", 64 * lo + 8, 64 * mid, 16))
+            for gi in even:
                 to_list(gi)
         yield out3
 
@@ -301,22 +305,23 @@ def rank_program(g, core, T, topo):
                 gap()
             else:
                 tt(A("nm", 48, 56), A("nw", 48, 56), A("offc", 48, 56), ALU.subtract)
-                turn(A("tr"), A("gt"))
                 tt(A("pn", 48, 56), A("nm", 48, 56), A("wv", 48, 56), ALU.mult)
+                turn(A("tr"), A("gt"))
+                tt(A("nn", 24, 28), A("pn", 48, 52), A("pn", 52, 56), ALU.add)
             tt(A("wv", a, a + 4), A("tr", s, 64, 16), A("tr", 64 + s, 128, 16), ALU.is_le)
             tt(A("wv", a + 4, a + 8), A("tr", s, 64, 16), A("tr", 64 + s, 128, 16), ALU.is_gt)
             if s == 7:
-                tt(A("nn", 24, 28), A("pn", 48, 52), A("pn", 52, 56), ALU.add)
+                copy(A("nbu", 24, 28), A("nn", 24, 28))
+                act(A("gf", 384, 448), A("win"), off=A("nbu", 24, 28))
                 tt(A("pn", 56, 64), A("wv", 56, 64), A("tr", 15, 128, 16), ALU.mult)
-                copy(A("nbu", 12, 16), A("nn", 24, 28))
-                act(A("gf", 192, 256), A("win"), off=A("nbu", 12, 16))
+                gap()
                 tt(A("nn", 28, 32), A("pn", 56, 60), A("pn", 60, 64), ALU.add)
                 gap()
                 copy(A("na", 28, 32), A("nn", 28, 32))
                 to_list(7)
-                turn(A("tf", 192, 256), A("gf", 192, 256))
+                turn(A("tf", 384, 448), A("gf", 384, 448))
                 gap()
-                copy(A("na", 24, 28), A("tf", 200, 256, 16))
+                copy(A("na", 24, 28), A("tf", 392, 448, 16))
                 to_list(6)
                 while todo:
                     gap()
@@ -329,8 +334,10 @@ def rank_program(g, core, T, topo):
             tt(A("nw", a, a + 8), A("pt"), base, ALU.add)
             gap()
             copy(A("ll"), A("nw", a, a + 8))
+            if s == 3:
+                todo.extend(batch((0, 2), (1, 3)))
             if s == 5:
-                todo.extend(batch())
+                todo.extend(batch((4,), (5,)))
 
     n_in_b = 2 * len(topo.engines(nxt, core))
     n_in_r = 2 * len(topo.engines(prv, core))
@@ -343,15 +350,14 @@ def rank_program(g, core, T, topo):
         for h in range(8):
             dma("y" if h < 4 else "s", "rl", A("win", p=(16 * h, 16 * h + 8)), A("sn", p=(0, 128, 16)))
         unpack((2, 3, 4, 5), 288, 416, "vvss", 32)
-        fill(A("inv0"), 1280.0)
-        fill(A("inv1"), 1280.0)
-        if r == 0:
-            constants()
+        for k in range(2):
+            act(A("inv%d" % k), A("iw"), AF.Identity, scale=0.0, bias=1280.0)
         growth()
         for t in (2, 3, 0, 1):
             ts(A("ml", 20 * t, 20 * t + 20), A("nl"), 4.0, ALU.mult, float(t), ALU.add)
         for t in (2, 3):
             act(A("mt", t, 1280, 4), A("vt"), off=A("ml", 20 * t, 20 * t + 20))
+        act(A("nr"), A("iw", 0, E), off=A("nl"))
         for t in (0, 1):
             pick(A("mt", t, 1280, 4), A("vt"), A("ml", 20 * t, 20 * t + 20))
         copy(A("nlf"), A("nl"))
@@ -361,7 +367,6 @@ def rank_program(g, core, T, topo):
             mm(hb[b], "w", 128 * b, "m", 0, 320)
         for b in range(4):
             act(A("tb", b, 1280, 4), P(hb[b], 0, 320), scale=0.03125)
-        pick(A("nr"), A("iw"), A("nl"))
         ts(A("tq"), A("nlf"), -1.0, ALU.mult, A("q4", 0, 1), ALU.add)
         tt(A("eq"), A("nlf"), A("nr"), ALU.is_equal, off=A("cidx"))
         if last:
@@ -371,32 +376,40 @@ def rank_program(g, core, T, topo):
         tt(A("dp"), A("dup"), A("tq"), ALU.mult)
         tt(A("ad"), A("nlf"), A("dp"), ALU.add)
         copy(A("adr", 0, 40, 2), A("ad"))
-        quant("t", 0, 320, A("tb"))
-        for b in range(4):
-            mm(2 + b, "e", 128 * b, "t", 0, 320)
-        for b in range(4):
-            act(A("tt", b, 1280, 4), P(2 + b, 0, 320), scale=-1.0)
         for c in range(9, -1, -1):
+            if c == 6:
+                quant("t", 0, 320, A("tb"))
+                for b in range(4):
+                    mm(2 + b, "e", 128 * b, "t", 0, 320)
+                for b in range(4):
+                    act(A("tt", b, 1280, 4), P(2 + b, 0, 320), scale=-1.0)
             for k in (1, 0):
                 d = 10 * k + c
                 put(A("inv%d" % k), A("adr", 2 * d, 2 * d + 1), A("jr", 16 * d, 16 * d + 16))
-        for k in (1, 0):
-            scan(A("dg%d" % k), A("dia"), A("inv%d" % k, 0, 416), ALU.add, ALU.max)
-        tt(A("dm"), A("dg0", 15, 416, 16), A("dg1", 15, 416, 16), ALU.min)
-        for t in (2, 3, 0, 1):
-            ts(A("ul", 26 * t, 26 * t + 26), A("dm"), A("hs", 0, 1), ALU.subtract, float(t), ALU.add)
+
+        def lists(lo, hi, out):
+            n = (hi - lo) // 16
+            for k in (1, 0):
+                scan(A("dg%d" % k, lo, hi), A("dia", lo, hi), A("inv%d" % k, lo, hi), ALU.add, ALU.max)
+            m = A("dm", lo // 16, hi // 16)
+            tt(m, A("dg0", lo + 15, hi, 16), A("dg1", lo + 15, hi, 16), ALU.min)
+            for t in (2, 3, 0, 1):
+                ts(A(out, n * t, n * t + n), m, A("hs", 0, 1), ALU.subtract, float(t), ALU.add)
+        lists(C, E, "ulb")
         for t in (2, 3):
-            act(A("ub", t, 384, 4), A("tt"), scale=-1.0, off=A("ul", 26 * t + 20, 26 * t + 26))
+            act(A("ub", t, 384, 4), A("tt"), scale=-1.0, off=A("ulb", 6 * t, 6 * t + 6))
         for t in (0, 1):
-            ts(A("ub", t, 384, 4), A("tt"), -1.0, ALU.mult, off=A("ul", 26 * t + 20, 26 * t + 26))
+            ts(A("ub", t, 384, 4), A("tt"), -1.0, ALU.mult, off=A("ulb", 6 * t, 6 * t + 6))
         quant("r", 0, 128, A("ub"))
         send(nxt, "r", 0, H, 128, "ra%d" % r, "rtl")
+        lists(0, C, "ul")
         for t in range(4):
-            tt(A("xt", 384 + t, 1280, 4), A("tt"), A("vt", 384 + t, 1280, 4), ALU.add, off=A("ul", 26 * t + 6, 26 * t + 20))
+            tt(A("xt", 384 + t, 1280, 4), A("tt"), A("vt", 384 + t, 1280, 4), ALU.add, off=A("ul", 20 * t + 6, 20 * t + 20))
         quant("c", 128, 320, A("xt", 512, 1280))
         for t in range(4):
-            tt(A("xf", t, 384, 4), A("tt"), A("vt", t, 384, 4), ALU.add, off=A("ul", 26 * t, 26 * t + 6))
+            tt(A("xf", t, 384, 4), A("tt"), A("vt", t, 384, 4), ALU.add, off=A("ul", 20 * t, 20 * t + 6))
         if last:
+            quant("v", 0, 128, A("vin"))
             mm(6, "v", 0, "c", 128, 320)
             act(A("ysb", 128, 320), P(6, 0, 192))
             dma("y", "ob", T.y[:, 128:320], A("ysb", 128, 320))

@@ -11,18 +11,17 @@ def _declare(kind, names):
         SCRATCH[n] = ("psum" if n.startswith("ps") else "sbuf", [128, int(c)], kind)
 
 
-_declare("bfloat16", "xt:1280 ut:512 vin:512 eb:516 vt:1664 mt:1280 tb:1280 tt:1296 ub:512")
+_declare("bfloat16", "xt:1280 ut:512 vin:512 eb:516 vt:1664 mt:1280 tb:1280 tt:1344 ub:512")
 _declare("int32", "lri:52 pi:8 pa:8 pb:8 pq:8")
-_declare("uint16", "lru:52 l0:8 ll:8 cidx:20 nbu:32 na:32 nl:20 ml:80 qrep:26 adr:40 ul:80 ulb:24")
-_declare("float8_e4m3fn_x4", "qw:512 qu:128 qv:128 qe:512 qc:416 qm:320 qt:320 qr:224")
-_declare("uint8", "sw:512 su:128 sv:128 se:512 sc:416 sm:320 st:320 sr:224")
-_declare("float32", "idn:516 iw:432 cs:96 dsc:320 dia:416 jr:320 offc:64 c16:8 pf:8 ja:8 jb:8 jc:8")
+_declare("uint16", "lru:52 l0:8 ll:8 cidx:20 nbu:32 na:32 nl:20 qrep:26 adr:40 ul:20 ulb:6 lz:8 lab:8 lt:8")
+_declare("float8_e4m3fn_x4", "qw:512 qu:128 q0:128 qv:128 qe:512 qc:416 qm:320 qt:320 qr:224")
+_declare("uint8", "sw:512 su:128 s0:128 sv:128 se:512 sc:416 sm:320 st:320 sr:224")
+_declare("float32", "idn:516 iw:416 cs:96 dsc:320 dia:416 offc:64 c16:8 pf:8 ja:8 jb:8 jc:8")
 _declare("float32", "k0:8 k1:8 k2:8 k3:8 k4:8 k5:8 hs:8 q4:8 dn:832 aiw:416 bi:832 win:832 ts0:128 gt:128 tr:128")
-_declare("float32", "wv:64 nw:64 pt:8 nm:64 pn:64 nn:32 gf:512 tf:512 nlf:20 ss:416 sn:832 nr:320 eq:320 scn:320 tq:20")
-_declare("float32", "dup:20 dp:20 ad:20 inv0:432 inv1:432 dg0:416 dg1:416 dm:26 xf:384 ysb:320")
+_declare("float32", "wv:64 nw:64 pt:8 nm:64 pn:64 nn:32 gf:512 tf:512 nlf:20 ss:416 s2:416 sn:832 nr:320 eq:320 scn:320")
+_declare("float32", "dq:20 ad:20 inv0:432 inv1:432 dg0:416 dg1:416 dm:26 xf:384 ysb:320")
 _declare("float32", "ps0:512 ps1:512 ps2:512 ps3:512 ps4:512 ps5:512 ps6:512 ps7:512")
 SEMAPHORES = "cv cs ct cg lx0 lx1 llr lu lv lw stc rl nd ob bl rtl ba0 ba1 ba2 ra0 ra1 ra2".split()
-POS = {0: 0, 2: 1, 1: 2, 3: 3, 4: 4, 5: 5, 6: 6, 7: 7}
 
 
 def rank_program(g, core, T, topo):
@@ -159,8 +158,8 @@ def rank_program(g, core, T, topo):
         oa, ia = [a["ap"] if isinstance(a, dict) else a for a in (out, i)]
         op(q, lambda: eng[q].dma_start(oa, ia), w, rd, sem=sem, inc=16)
 
-    def iota(o, pattern, cm):
-        op("g", lambda: g.iota(o["ap"], pattern, 0, cm, allow_small_or_imprecise_dtypes=True), [o], [])
+    def iota(o, pattern, cm, base=0):
+        op("g", lambda: g.iota(o["ap"], pattern, base, cm, allow_small_or_imprecise_dtypes=True), [o], [])
 
     def send(dst, k, a, b, c, rsem, lsem):
         rid, pid = topo.addr(dst)[:2]
@@ -173,12 +172,15 @@ def rank_program(g, core, T, topo):
         for b in range(4):
             mm(banks[b], "e", 128 * b, "c", lo, hi)
         for b in range(4):
-            o, i = A("vt", 4 * (lo + skip) + b, 4 * hi, 4), P(banks[b], skip, hi - lo)
+            o, i = A("vt", E * b + lo + skip, E * b + hi), P(banks[b], skip, hi - lo)
             copy(o, i) if who[b] == "v" else act(o, i)
 
-    def score(bank, lo, hi, skip=0):
+    def score(bank, bank2, lo, hi, skip=0, both=True):
         mm(bank, "u", 0, "c", lo, hi)
+        mm(bank2, "0", 0, "c", lo, hi)
         act(A("ss", lo + skip, hi), P(bank, skip, hi - lo), AF.Abs)
+        if both:
+            act(A("s2", lo + skip, hi), P(bank2, skip, hi - lo), AF.Abs)
 
     def border_out(r):
         send(prv, "c", 0, H, C, "ba%d" % r, "bl")
@@ -194,9 +196,11 @@ def rank_program(g, core, T, topo):
     pi = A("pi")
     op("g", lambda: g.iota(pi["ap"], [[0, 8]], 0, 1), [pi], [])
     iota(A("c16"), [[416, 2], [256, 2], [16, 2]], 0)
-    iota(A("iw"), [[1, 432]], 0)
-    iota(A("idn"), [[1, 516]], -4)
+    iota(A("iw"), [[1, 416]], 0)
     iota(A("offc"), [[0, 8], [416, 2], [0, 4]], 0)
+    quant("c", 0, 128, A("xt", 0, 512))
+    border_out(0)
+    iota(A("idn"), [[1, 516]], -4)
 
     z, q = A("k0", 0, 1), A("pf", 1, 2)
     copy(A("pf", 0, 1), A("pi", 0, 1))
@@ -217,7 +221,7 @@ def rank_program(g, core, T, topo):
     ts(A("ja"), A("pa"), 32.0, ALU.mult)
     ts(A("q4", 0, 1), q, 416.0, ALU.add)
     tt(A("jb"), A("ja"), A("pb"), ALU.add)
-    fill(A("tt", 1280, 1296), 0.0)
+    fill(A("lz"), 0)
     tt(A("jc"), A("jb"), A("c16"), ALU.add)
     fill(A("ub", 384, 512), 0.0)
     copy(A("l0"), A("jc"))
@@ -232,73 +236,81 @@ def rank_program(g, core, T, topo):
     ts(d16, d16, 1.0, ALU.add)
     copy(A("cidx"), A("iw", 0, 20))
     tt(A("cs", 0, 16), d16, A("cs", 80, 96), ALU.mult)
-    ts(A("eb"), A("idn"), 3.0, ALU.is_equal)
-    w16 = A("iw", 0, E)
+    w16 = A("iw")
     act(A("aiw"), w16, scale=A("k2", 0, 1))
     act(A("bi", 0, 416), w16, scale=A("k4", 0, 1))
     act(A("bi", 416, 832), w16, AF.Identity, scale=A("k4", 0, 1), bias=A("k5", 0, 1))
-    act(A("jr"), A("iw", 0, 320), scale=4.0)
     act(A("dsc"), A("cs", 0, 16), off=A("qrep", 0, 20))
     act(A("dia"), A("cs", 16, 32), off=A("qrep", 0, 26))
 
-    quant("c", 0, 128, A("xt", 0, 512))
-    border_out(0)
     copy(A("lru"), A("lri"))
-    quant("u", 0, 128, A("ut"))
-    score(0, 0, 128)
     tt(A("dn"), A("aiw"), A("bi"), ALU.add, off=A("lru"))
     for h in range(8):
         for k in range(2):
             dma("y" if h < 5 else "s", "stc", A("win", p=(16 * h + 8 * k, 16 * h + 8 * k + 8)), A("dn", p=(1 - k, 128, 16)))
+    quant("u", 0, 128, A("ut"))
+    for n, w in (("q", dt.uint32), ("s", None)):
+        pick(A(n + "0", bits=w), A(n + "u", bits=w), A("lz"))
+    score(0, 1, 0, 128)
     quant("c", 128, 320, A("xt", 512, 1280))
-    score(6, 128, 320)
+    score(6, 7, 128, 320)
+    for b in range(4):
+        fill(A("tt", 336 * b + 320, 336 * b + 336), 0.0)
+    ts(A("eb"), A("idn"), 3.0, ALU.is_equal)
     for b in range(4):
         quant("e", 128 * b, 128 * b + 128, A("eb", 3 - b, 515 - b))
-    unpack((2, 3, 4, 5), 0, 128, "vvss")
-    unpack((7, 1, 2, 3), 128, 320, "ssss")
     pick(A("gt"), A("win"), A("l0"))
     turn(A("ts0"), A("gt"))
+    tt(A("pt"), A("ts0", 0, 128, 16), A("ts0", 8, 128, 16), ALU.add)
+    copy(A("lt"), A("pt"))
+    pick(A("gt"), A("win"), A("lt"))
+    turn(A("tr"), A("gt"))
+    tt(A("pt"), A("tr", 8, 128, 16), A("offc", 0, 8), ALU.subtract)
+    copy(A("lab"), A("pt"))
 
-    def to_list(gi):
-        c, p = 4 * POS[gi], (16 * gi, 16 * gi + 16)
-        dma("y", "nd", A("nl", 0, 16, p=p), A("na", c, c + 2))
-        dma("y", "nd", A("nl", 16, 20, p=p), A("na", c + 2, c + 4, p=(0, 32)))
+    def to_list(gi, q="y"):
+        c, p = 4 * gi, (16 * gi, 16 * gi + 16)
+        dma(q, "nd", A("nl", 0, 16, p=p), A("na", c, c + 2))
+        dma(q, "nd", A("nl", 16, 20, p=p), A("na", c + 2, c + 4, p=(0, 32)))
 
-    def batch(even, odd):
-        lo, k = POS[even[0]], len(even)
-        mid, hi = lo + k, lo + 2 * k
-        yield lambda: tt(A("nm", 8 * lo, 8 * hi), A("nw", 8 * lo, 8 * hi), A("offc", 8 * lo, 8 * hi), ALU.subtract)
-        yield lambda: tt(A("pn", 8 * lo, 8 * hi), A("nm", 8 * lo, 8 * hi), A("wv", 8 * lo, 8 * hi), ALU.mult)
-        for s in range(lo, hi):
-            yield lambda s=s: tt(A("nn", 4 * s, 4 * s + 4), A("pn", 8 * s, 8 * s + 4), A("pn", 8 * s + 4, 8 * s + 8), ALU.add)
+    def choices(s):
+        a, b = 8 * s, 8 * s + 16
+        m = 4 * s
+        yield lambda: tt(A("nm", a, b), A("nw", a, b), A("offc", a, b), ALU.subtract)
+        yield lambda: tt(A("pn", a, b), A("nm", a, b), A("wv", a, b), ALU.mult)
+        yield lambda: tt(A("nn", m, m + 4), A("pn", a, a + 4), A("pn", a + 4, a + 8), ALU.add)
+        yield lambda: tt(A("nn", m + 4, m + 8), A("pn", a + 8, a + 12), A("pn", a + 12, a + 16), ALU.add)
 
         def out():
-            copy(A("nbu", 4 * lo, 4 * mid), A("nn", 4 * lo, 4 * mid))
-            act(A("gf", 64 * lo, 64 * mid), A("win"), off=A("nbu", 4 * lo, 4 * mid))
+            copy(A("nbu", m, m + 4), A("nn", m, m + 4))
+            act(A("gf", 16 * m, 16 * m + 64), A("win"), off=A("nbu", m, m + 4))
         yield out
 
         def out2():
-            copy(A("na", 4 * mid, 4 * hi), A("nn", 4 * mid, 4 * hi))
-            for gi in odd:
-                to_list(gi)
+            copy(A("na", m + 4, m + 8), A("nn", m + 4, m + 8))
+            to_list(s + 1)
         yield out2
-        yield lambda: turn(A("tf", 64 * lo, 64 * mid), A("gf", 64 * lo, 64 * mid))
+        yield None
+        yield lambda: turn(A("tf", 16 * m, 16 * m + 64), A("gf", 16 * m, 16 * m + 64))
 
         def out3():
-            copy(A("na", 4 * lo, 4 * mid), A("tf", 64 * lo + 8, 64 * mid, 16))
-            for gi in even:
-                to_list(gi)
+            copy(A("na", m, m + 4), A("tf", 16 * m + 8, 16 * m + 64, 16))
+            to_list(s)
         yield out3
 
     def growth():
         todo = []
 
         def gap():
-            if todo:
-                todo.pop(0)()
+            f = todo.pop(0) if todo else None
+            if f:
+                f()
         for s in range(8):
-            a = 8 * POS[s]
-            pick(A("gt"), A("win"), A("l0") if s == 0 else A("ll"))
+            a = 8 * s
+            if s == 0:
+                pick(A("gt"), A("s2"), A("lab"))
+            else:
+                pick(A("gt"), A("win"), A("ll"))
             if s < 7:
                 gap()
                 turn(A("tr"), A("gt"))
@@ -322,7 +334,7 @@ def rank_program(g, core, T, topo):
                 turn(A("tf", 384, 448), A("gf", 384, 448))
                 gap()
                 copy(A("na", 24, 28), A("tf", 392, 448, 16))
-                to_list(6)
+                to_list(6, "s")
                 while todo:
                     gap()
                 break
@@ -334,32 +346,32 @@ def rank_program(g, core, T, topo):
             tt(A("nw", a, a + 8), A("pt"), base, ALU.add)
             gap()
             copy(A("ll"), A("nw", a, a + 8))
-            if s == 3:
-                todo.extend(batch((0, 2), (1, 3)))
-            if s == 5:
-                todo.extend(batch((4,), (5,)))
+            if s in (1, 3, 5):
+                todo.extend(choices(s - 1))
 
     n_in_b = 2 * len(topo.engines(nxt, core))
     n_in_r = 2 * len(topo.engines(prv, core))
     for r in range(ROUNDS):
         last = r == ROUNDS - 1
         arrive("ba%d" % r, n_in_b, [A("qc", C, E), A("sc", C, E)])
-        score(1, 288, 416, 32)
-        pick(A("sn", 0, 416), A("ss"), A("lru", 0, 26))
-        act(A("sn", 416, 832), A("ss"), off=A("lru", 26, 52))
+        score(6, 7, 288, 416, 32, False)
+        pick(A("sn", 0, 480), A("ss"), A("lru", 0, 30))
+        act(A("sn", 480, 832), A("ss"), off=A("lru", 30, 52))
+        act(A("s2", C, E), P(7, 32, 128), AF.Abs)
         for h in range(8):
             dma("y" if h < 4 else "s", "rl", A("win", p=(16 * h, 16 * h + 8)), A("sn", p=(0, 128, 16)))
-        unpack((2, 3, 4, 5), 288, 416, "vvss", 32)
+        if r == 0:
+            unpack((2, 3, 4, 5), 0, 128, "ssss")
+            unpack((0, 1, 2, 3), 128, 320, "ssss")
+        unpack((2, 3, 4, 5), 288, 416, "ssss", 32)
         for k in range(2):
-            act(A("inv%d" % k), A("iw"), AF.Identity, scale=0.0, bias=1280.0)
+            iota(A("inv%d" % k), [[0, 432]], 0, base=320)
         growth()
-        for t in (2, 3, 0, 1):
-            ts(A("ml", 20 * t, 20 * t + 20), A("nl"), 4.0, ALU.mult, float(t), ALU.add)
         for t in (2, 3):
-            act(A("mt", t, 1280, 4), A("vt"), off=A("ml", 20 * t, 20 * t + 20))
-        act(A("nr"), A("iw", 0, E), off=A("nl"))
+            act(A("mt", t, 1280, 4), A("vt", E * t, E * t + E), off=A("nl"))
+        act(A("nr"), A("iw"), off=A("nl"))
         for t in (0, 1):
-            pick(A("mt", t, 1280, 4), A("vt"), A("ml", 20 * t, 20 * t + 20))
+            pick(A("mt", t, 1280, 4), A("vt", E * t, E * t + E), A("nl"))
         copy(A("nlf"), A("nl"))
         quant("m", 0, 320, A("mt"))
         hb = (0, 1, 6, 7)
@@ -367,14 +379,12 @@ def rank_program(g, core, T, topo):
             mm(hb[b], "w", 128 * b, "m", 0, 320)
         for b in range(4):
             act(A("tb", b, 1280, 4), P(hb[b], 0, 320), scale=0.03125)
-        ts(A("tq"), A("nlf"), -1.0, ALU.mult, A("q4", 0, 1), ALU.add)
         tt(A("eq"), A("nlf"), A("nr"), ALU.is_equal, off=A("cidx"))
         if last:
             dma("y", "ob", T.on[:, :], A("nr", p=(0, 128, 16)))
         scan(A("scn"), A("dsc"), A("eq"), ALU.mult, ALU.add)
-        ts(A("dup"), A("scn", 15, 320, 16), 32.0, ALU.is_ge)
-        tt(A("dp"), A("dup"), A("tq"), ALU.mult)
-        tt(A("ad"), A("nlf"), A("dp"), ALU.add)
+        ts(A("dq"), A("scn", 15, 320, 16), 32.0, ALU.is_ge, A("q4", 0, 1), ALU.mult)
+        tt(A("ad"), A("nlf"), A("dq"), ALU.max)
         copy(A("adr", 0, 40, 2), A("ad"))
         for c in range(9, -1, -1):
             if c == 6:
@@ -382,46 +392,47 @@ def rank_program(g, core, T, topo):
                 for b in range(4):
                     mm(2 + b, "e", 128 * b, "t", 0, 320)
                 for b in range(4):
-                    act(A("tt", b, 1280, 4), P(2 + b, 0, 320), scale=-1.0)
+                    act(A("tt", 336 * b, 336 * b + 320), P(2 + b, 0, 320), scale=-1.0)
             for k in (1, 0):
                 d = 10 * k + c
-                put(A("inv%d" % k), A("adr", 2 * d, 2 * d + 1), A("jr", 16 * d, 16 * d + 16))
+                put(A("inv%d" % k), A("adr", 2 * d, 2 * d + 1), A("iw", 16 * d, 16 * d + 16))
 
         def lists(lo, hi, out):
-            n = (hi - lo) // 16
             for k in (1, 0):
                 scan(A("dg%d" % k, lo, hi), A("dia", lo, hi), A("inv%d" % k, lo, hi), ALU.add, ALU.max)
             m = A("dm", lo // 16, hi // 16)
             tt(m, A("dg0", lo + 15, hi, 16), A("dg1", lo + 15, hi, 16), ALU.min)
-            for t in (2, 3, 0, 1):
-                ts(A(out, n * t, n * t + n), m, A("hs", 0, 1), ALU.subtract, float(t), ALU.add)
+            ts(A(out), m, A("hs", 0, 1), ALU.subtract)
+
+        def minus(t):
+            return A("tt", 336 * t, 336 * t + 336)
         lists(C, E, "ulb")
         for t in (2, 3):
-            act(A("ub", t, 384, 4), A("tt"), scale=-1.0, off=A("ulb", 6 * t, 6 * t + 6))
+            act(A("ub", t, 384, 4), minus(t), scale=-1.0, off=A("ulb"))
         for t in (0, 1):
-            ts(A("ub", t, 384, 4), A("tt"), -1.0, ALU.mult, off=A("ulb", 6 * t, 6 * t + 6))
+            ts(A("ub", t, 384, 4), minus(t), -1.0, ALU.mult, off=A("ulb"))
         quant("r", 0, 128, A("ub"))
         send(nxt, "r", 0, H, 128, "ra%d" % r, "rtl")
         lists(0, C, "ul")
         for t in range(4):
-            tt(A("xt", 384 + t, 1280, 4), A("tt"), A("vt", 384 + t, 1280, 4), ALU.add, off=A("ul", 20 * t + 6, 20 * t + 20))
+            tt(A("xt", 384 + t, 1280, 4), minus(t), A("vt", E * t + H, E * t + C), ALU.add, off=A("ul", 6, 20))
         quant("c", 128, 320, A("xt", 512, 1280))
         for t in range(4):
-            tt(A("xf", t, 384, 4), A("tt"), A("vt", t, 384, 4), ALU.add, off=A("ul", 20 * t, 20 * t + 6))
+            tt(A("xf", H * t, H * t + H), minus(t), A("vt", E * t, E * t + H), ALU.add, off=A("ul", 0, 6))
         if last:
             quant("v", 0, 128, A("vin"))
             mm(6, "v", 0, "c", 128, 320)
             act(A("ysb", 128, 320), P(6, 0, 192))
             dma("y", "ob", T.y[:, 128:320], A("ysb", 128, 320))
         else:
-            score(6, 128, 320)
+            score(6, 7, 128, 320)
             unpack((2, 3, 4, 5), 128, 320, "ssss")
         arrive("ra%d" % r, n_in_r, [A("qr", 128, 224), A("sr", 128, 224)])
         bb = (0, 1, 7, 6)
         for b in range(4):
             mm(bb[b], "e", 128 * b, "r", 96, 224)
         for b in range(4):
-            tt(A("xt", b, 384, 4), A("xf", b, 384, 4), P(bb[b], 32, 128), ALU.subtract)
+            tt(A("xt", b, 384, 4), A("xf", H * b, H * b + H), P(bb[b], 32, 128), ALU.subtract)
         quant("c", 0, 128, A("xt", 0, 512))
         if last:
             mm(0, "v", 0, "c", 0, 128)
@@ -432,7 +443,7 @@ def rank_program(g, core, T, topo):
             dma("s", "ob", T.y[:, 0:128], A("ysb", 0, 128))
         else:
             border_out(r + 1)
-            score(0, 0, 128)
+            score(0, 1, 0, 128)
             unpack((2, 3, 4, 5), 0, 128, "vvss")
     for s in SEMAPHORES:
         if know["g"].get(s, 0) < cnt[s]:

from concourse.mybir import dt, AluOpType as ALU, ActivationFunctionType as AF

ROUNDS = 3
C, H, E = 320, 96, 416
SCRATCH = {}


def _declare(kind, names):
    for w in names.split():
        n, c = w.split(":")
        SCRATCH[n] = ("psum" if n.startswith("ps") else "sbuf", [128, int(c)], kind)


_declare("bfloat16", "xt:1280 ut:512 vin:512 eb:516 vt:1664 mt:1280 tb:1280 tt:1344 ub:512")
_declare("int32", "lri:52 pi:8 pa:8 pb:8 pq:8")
_declare("uint16", "lru:52 l0:8 ll:8 cidx:20 nbu:32 na:32 nl:20 qrep:26 adr:40 ul:20 ulb:6 lz:8 lab:8 lt:8")
_declare("float8_e4m3fn_x4", "qw:512 qu:128 q0:128 qv:128 qe:512 qc:416 qm:320 qt:320 qr:224")
_declare("uint8", "sw:512 su:128 s0:128 sv:128 se:512 sc:416 sm:320 st:320 sr:224")
_declare("float32", "idn:516 iw:416 cs:96 dsc:320 dia:416 offc:64 c16:8 pf:8 ja:8 jb:8 jc:8")
_declare("float32", "k0:8 k1:8 k2:8 k3:8 k4:8 k5:8 hs:8 q4:8 dn:832 aiw:416 bi:832 win:832 ts0:128 gt:128 tr:128")
_declare("float32", "wv:64 nw:64 pt:8 nm:64 pn:64 nn:32 gf:512 tf:512 nlf:20 ss:416 s2:416 sn:832 nr:320 eq:320 scn:320")
_declare("float32", "dq:20 ad:20 inv0:432 inv1:432 dg0:416 dg1:416 dm:26 xf:384 ysb:320")
_declare("float32", "ps0:512 ps1:512 ps2:512 ps3:512 ps4:512 ps5:512 ps6:512 ps7:512")
SEMAPHORES = "cv cs ct cg lx0 lx1 llr lu lv lw stc rl nd ob bl rtl ba0 ba1 ba2 ra0 ra1 ra2".split()


def rank_program(g, core, T, topo):
    rank = T.rank_of(core)
    if rank is None:
        return
    nxt, prv = T.cores[(rank + 1) % 4], T.cores[(rank - 1) % 4]
    eng = {"v": g.vector, "s": g.scalar, "t": g.tensor, "g": g, "y": g.sync}
    csem = {"v": "cv", "s": "cs", "t": "ct", "g": "cg"}
    cnt = {s: 0 for s in SEMAPHORES}
    know = {q: {} for q in eng}
    acc = {}
    serial = [0]

    def A(name, lo=0, hi=None, step=1, p=None, bits=None):
        t = T[name]
        hi = t.shape[1] if hi is None else hi
        ps = slice(None) if p is None else slice(*p)
        ap = t[ps, lo:hi] if step == 1 else t[ps, lo:hi:step]
        if bits is not None:
            ap = ap.bitcast(bits)
        p0, p1 = (0, 128) if p is None else (p[0], p[1])
        return {"ap": ap, "n": name, "lo": lo, "hi": hi, "st": step, "p0": p0, "p1": p1}

    def meet(a, b):
        if a["n"].startswith("ps"):
            return True
        if a["hi"] <= b["lo"] or b["hi"] <= a["lo"] or a["p1"] <= b["p0"] or b["p1"] <= a["p0"]:
            return False
        return not (a["st"] == b["st"] and a["st"] > 1 and (a["lo"] - b["lo"]) % a["st"])

    def learn(q, rec, val):
        k = know[q]
        k[rec["sem"]] = max(k.get(rec["sem"], 0), val)
        for s, c in rec["know"].items():
            if k.get(s, 0) < c:
                k[s] = c

    def settle(q, reads, writes):
        need = []
        for kind, regs in ((0, reads), (1, writes)):
            for r in regs:
                for a in acc.get(r["n"], []):
                    if not meet(r, a["reg"]):
                        continue
                    same = a["rec"]["q"] == q and not a["rec"]["late"]
                    if kind == 0 and not a["w"] and (same or not r["n"].startswith("ps")):
                        continue
                    need.append(a["rec"])
        need.sort(key=lambda rec: -rec["id"])
        for rec in need:
            if know[q].get(rec["sem"], 0) >= rec["val"]:
                continue
            val = cnt[rec["sem"]] if rec["late"] else rec["val"]
            eng[q].wait_ge(T.sem[rec["sem"]], val)
            learn(q, rec, val)

    def note(rec, reads, writes):
        for w, regs in ((False, reads), (True, writes)):
            for r in regs:
                old = acc.get(r["n"], [])
                if w and r["st"] == 1:
                    old = [a for a in old if not (a["reg"]["lo"] >= r["lo"] and a["reg"]["hi"] <= r["hi"] and a["reg"]["p0"] >= r["p0"] and a["reg"]["p1"] <= r["p1"])]
                old.append({"reg": r, "rec": rec, "w": w})
                acc[r["n"]] = old

    def op(q, fn, writes, reads, sem=None, inc=1, self_inc=False):
        settle(q, reads, writes)
        s = sem or csem[q]
        ins = fn()
        if not self_inc:
            ins.then_inc(T.sem[s], inc)
        cnt[s] += inc
        serial[0] += 1
        note({"q": q, "sem": s, "val": cnt[s], "late": sem is not None, "know": dict(know[q]), "id": serial[0]}, reads, writes)

    def arrive(sem, n, writes):
        cnt[sem] += n
        serial[0] += 1
        note({"q": "far", "sem": sem, "val": cnt[sem], "late": True, "know": {}, "id": serial[0]}, [], writes)

    def copy(out, i):
        op("v", lambda: g.vector.tensor_copy(out["ap"], i["ap"]), [out], [i])

    def pick(out, i, off):
        op("v", lambda: g.vector.tensor_copy(out["ap"], i["ap"].indirect(off["ap"])), [out], [i, off])

    def put(out, off, i):
        op("v", lambda: g.vector.tensor_copy(out["ap"].indirect(off["ap"]), i["ap"]), [out], [off, i])

    def tt(out, a, b, o, off=None):
        ia = a["ap"] if off is None else a["ap"].indirect(off["ap"])
        op("v", lambda: g.vector.tensor_tensor(out["ap"], ia, b["ap"], o), [out], [a, b] + ([off] if off else []))

    def ts(out, a, s1, o1, s2=None, o2=None, off=None):
        ia = a["ap"] if off is None else a["ap"].indirect(off["ap"])
        rd = [a] + [s for s in (s1, s2, off) if isinstance(s, dict)]
        v1 = s1["ap"] if isinstance(s1, dict) else s1
        v2 = s2["ap"] if isinstance(s2, dict) else s2
        if o2 is None:
            op("v", lambda: g.vector.tensor_scalar(out["ap"], ia, v1, None, o1), [out], rd)
        else:
            op("v", lambda: g.vector.tensor_scalar(out["ap"], ia, v1, v2, o1, o2), [out], rd)

    def scan(out, d0, d1, o0, o1):
        op("v", lambda: g.vector.tensor_tensor_scan(out["ap"], d0["ap"], d1["ap"], 0.0, o0, o1), [out], [d0, d1])

    def turn(out, i):
        op("v", lambda: g.vector.transpose(out["ap"], i["ap"]), [out], [i])

    def fill(out, c):
        op("v", lambda: g.vector.memset(out["ap"], c), [out], [])

    def act(out, i, func=AF.Copy, scale=1.0, off=None, bias=0.0):
        ia = i["ap"] if off is None else i["ap"].indirect(off["ap"])
        sv, bv = [s["ap"] if isinstance(s, dict) else s for s in (scale, bias)]
        rd = [i] + [s for s in (off, scale, bias) if isinstance(s, dict)]
        op("s", lambda: g.scalar.activation(out["ap"], ia, func, scale=sv, bias=bv), [out], rd)

    def quant(k, lo, hi, src):
        o, s = A("q" + k, lo, hi), A("s" + k, lo, hi)
        op("v", lambda: g.vector.quantize_mx(o["ap"], s["ap"], src["ap"]), [o, s], [src])

    def mm(bank, w, wlo, x, lo, hi):
        o = A("ps%d" % bank, 0, hi - lo)
        a, b, c, d = A("q" + w, wlo, wlo + 128), A("s" + w, wlo, wlo + 128), A("q" + x, lo, hi), A("s" + x, lo, hi)
        op("t", lambda: g.tensor.matmul_mx(o["ap"], a["ap"], b["ap"], c["ap"], d["ap"], True, True), [o], [a, b, c, d])

    def P(bank, lo, hi):
        return A("ps%d" % bank, lo, hi)

    def dma(q, sem, out, i):
        w, rd = [[a] if isinstance(a, dict) else [] for a in (out, i)]
        oa, ia = [a["ap"] if isinstance(a, dict) else a for a in (out, i)]
        op(q, lambda: eng[q].dma_start(oa, ia), w, rd, sem=sem, inc=16)

    def iota(o, pattern, cm, base=0):
        op("g", lambda: g.iota(o["ap"], pattern, base, cm, allow_small_or_imprecise_dtypes=True), [o], [])

    def send(dst, k, a, b, c, rsem, lsem):
        rid, pid = topo.addr(dst)[:2]
        mask, n = topo.mask(core, dst), len(topo.engines(core, dst))
        for name, bits in (("q" + k, dt.uint8), ("s" + k, None)):
            i, o = A(name, a, b, bits=bits), A(name, c, c + b - a, bits=bits)
            op("g", lambda: g.remote_dma(o["ap"], i["ap"], T.sem[rsem], T.sem[lsem], pid, rid, mask), [], [i], sem=lsem, inc=n, self_inc=True)

    def unpack(banks, lo, hi, who, skip=0):
        for b in range(4):
            mm(banks[b], "e", 128 * b, "c", lo, hi)
        for b in range(4):
            o, i = A("vt", E * b + lo + skip, E * b + hi), P(banks[b], skip, hi - lo)
            copy(o, i) if who[b] == "v" else act(o, i)

    def score(bank, bank2, lo, hi, skip=0, both=True):
        mm(bank, "u", 0, "c", lo, hi)
        mm(bank2, "0", 0, "c", lo, hi)
        act(A("ss", lo + skip, hi), P(bank, skip, hi - lo), AF.Abs)
        if both:
            act(A("s2", lo + skip, hi), P(bank2, skip, hi - lo), AF.Abs)

    def border_out(r):
        send(prv, "c", 0, H, C, "ba%d" % r, "bl")

    dma("y", "lx0", A("xt", 0, 512), T.x[:, 0:512])
    dma("s", "llr", A("lri", 0, 26), T.lf[:, :])
    dma("y", "lx1", A("xt", 512, 1280), T.x[:, 512:1280])
    dma("s", "llr", A("lri", 26, 52), T.rt[:, :])
    dma("y", "lu", A("ut"), T.u[:, :])
    dma("s", "lw", A("qw", bits=dt.uint8), T.wc[:, :])
    dma("s", "lw", A("sw"), T.ws[:, :])
    dma("y", "lv", A("vin"), T.v[:, :])
    pi = A("pi")
    op("g", lambda: g.iota(pi["ap"], [[0, 8]], 0, 1), [pi], [])
    iota(A("c16"), [[416, 2], [256, 2], [16, 2]], 0)
    iota(A("iw"), [[1, 416]], 0)
    iota(A("offc"), [[0, 8], [416, 2], [0, 4]], 0)
    quant("c", 0, 128, A("xt", 0, 512))
    border_out(0)
    iota(A("idn"), [[1, 516]], -4)

    z, q = A("k0", 0, 1), A("pf", 1, 2)
    copy(A("pf", 0, 1), A("pi", 0, 1))
    ts(A("pq", 0, 1), A("pi", 0, 1), 15, ALU.bitwise_and)
    ts(z, A("pf", 0, 1), 0.0, ALU.is_equal)
    ts(A("k1", 0, 1), A("pf", 0, 1), 112.0, ALU.is_equal)
    copy(q, A("pq", 0, 1))
    ts(A("k2", 0, 1), z, -1.0, ALU.mult, 1.0, ALU.add)
    ts(A("k3", 0, 1), z, 2.0, ALU.mult, -1.0, ALU.add)
    ts(A("k5", 0, 1), z, 416.0, ALU.mult)
    tt(A("k4", 0, 1), A("k3", 0, 1), A("k1", 0, 1), ALU.add)
    for lo in (0, 4):
        ts(A("pa", lo, lo + 2), A("pi", lo, lo + 2), 7, ALU.bitwise_and)
        ts(A("pb", lo, lo + 2), A("pi", lo, lo + 2), 3, ALU.logical_shift_right)
        ts(A("pa", lo + 2, lo + 4), A("pi", lo + 2, lo + 4), 1, ALU.bitwise_and)
        ts(A("pb", lo + 2, lo + 4), A("pi", lo + 2, lo + 4), 1, ALU.logical_shift_right)
    ts(A("hs", 0, 1), q, 15.0, ALU.is_lt, 2000.0, ALU.mult)
    ts(A("ja"), A("pa"), 32.0, ALU.mult)
    ts(A("q4", 0, 1), q, 416.0, ALU.add)
    tt(A("jb"), A("ja"), A("pb"), ALU.add)
    fill(A("lz"), 0)
    tt(A("jc"), A("jb"), A("c16"), ALU.add)
    fill(A("ub", 384, 512), 0.0)
    copy(A("l0"), A("jc"))
    t16, d16 = A("iw", 0, 16), A("cs", 32, 48)
    ts(d16, t16, q, ALU.subtract)
    ts(A("cs", 80, 96), t16, 0.0, ALU.is_gt)
    ts(A("qrep"), A("iw", 0, 26), 0.0, ALU.mult, q, ALU.add)
    ts(A("cs", 48, 64), d16, 0.0, ALU.is_equal, -4000.0, ALU.mult)
    ts(A("cs", 64, 80), d16, 1.0, ALU.is_equal, 2000.0, ALU.mult)
    ts(d16, d16, 0.0, ALU.is_equal, 63.0, ALU.mult)
    tt(A("cs", 16, 32), A("cs", 48, 64), A("cs", 64, 80), ALU.add)
    ts(d16, d16, 1.0, ALU.add)
    copy(A("cidx"), A("iw", 0, 20))
    tt(A("cs", 0, 16), d16, A("cs", 80, 96), ALU.mult)
    w16 = A("iw")
    act(A("aiw"), w16, scale=A("k2", 0, 1))
    act(A("bi", 0, 416), w16, scale=A("k4", 0, 1))
    act(A("bi", 416, 832), w16, AF.Identity, scale=A("k4", 0, 1), bias=A("k5", 0, 1))
    act(A("dsc"), A("cs", 0, 16), off=A("qrep", 0, 20))
    act(A("dia"), A("cs", 16, 32), off=A("qrep", 0, 26))

    copy(A("lru"), A("lri"))
    tt(A("dn"), A("aiw"), A("bi"), ALU.add, off=A("lru"))
    for h in range(8):
        for k in range(2):
            dma("y" if h < 5 else "s", "stc", A("win", p=(16 * h + 8 * k, 16 * h + 8 * k + 8)), A("dn", p=(1 - k, 128, 16)))
    quant("u", 0, 128, A("ut"))
    for n, w in (("q", dt.uint32), ("s", None)):
        pick(A(n + "0", bits=w), A(n + "u", bits=w), A("lz"))
    score(0, 1, 0, 128)
    quant("c", 128, 320, A("xt", 512, 1280))
    score(6, 7, 128, 320)
    for b in range(4):
        fill(A("tt", 336 * b + 320, 336 * b + 336), 0.0)
    ts(A("eb"), A("idn"), 3.0, ALU.is_equal)
    for b in range(4):
        quant("e", 128 * b, 128 * b + 128, A("eb", 3 - b, 515 - b))
    pick(A("gt"), A("win"), A("l0"))
    turn(A("ts0"), A("gt"))
    tt(A("pt"), A("ts0", 0, 128, 16), A("ts0", 8, 128, 16), ALU.add)
    copy(A("lt"), A("pt"))
    pick(A("gt"), A("win"), A("lt"))
    turn(A("tr"), A("gt"))
    tt(A("pt"), A("tr", 8, 128, 16), A("offc", 0, 8), ALU.subtract)
    copy(A("lab"), A("pt"))

    def to_list(gi, q="y"):
        c, p = 4 * gi, (16 * gi, 16 * gi + 16)
        dma(q, "nd", A("nl", 0, 16, p=p), A("na", c, c + 2))
        dma(q, "nd", A("nl", 16, 20, p=p), A("na", c + 2, c + 4, p=(0, 32)))

    def choices(s):
        a, b = 8 * s, 8 * s + 16
        m = 4 * s
        yield lambda: tt(A("nm", a, b), A("nw", a, b), A("offc", a, b), ALU.subtract)
        yield lambda: tt(A("pn", a, b), A("nm", a, b), A("wv", a, b), ALU.mult)
        yield lambda: tt(A("nn", m, m + 4), A("pn", a, a + 4), A("pn", a + 4, a + 8), ALU.add)
        yield lambda: tt(A("nn", m + 4, m + 8), A("pn", a + 8, a + 12), A("pn", a + 12, a + 16), ALU.add)

        def out():
            copy(A("nbu", m, m + 4), A("nn", m, m + 4))
            act(A("gf", 16 * m, 16 * m + 64), A("win"), off=A("nbu", m, m + 4))
        yield out

        def out2():
            copy(A("na", m + 4, m + 8), A("nn", m + 4, m + 8))
            to_list(s + 1)
        yield out2
        yield None
        yield lambda: turn(A("tf", 16 * m, 16 * m + 64), A("gf", 16 * m, 16 * m + 64))

        def out3():
            copy(A("na", m, m + 4), A("tf", 16 * m + 8, 16 * m + 64, 16))
            to_list(s)
        yield out3

    def growth():
        todo = []

        def gap():
            f = todo.pop(0) if todo else None
            if f:
                f()
        for s in range(8):
            a = 8 * s
            if s == 0:
                pick(A("gt"), A("s2"), A("lab"))
            else:
                pick(A("gt"), A("win"), A("ll"))
            if s < 7:
                gap()
                turn(A("tr"), A("gt"))
                gap()
            else:
                tt(A("nm", 48, 56), A("nw", 48, 56), A("offc", 48, 56), ALU.subtract)
                tt(A("pn", 48, 56), A("nm", 48, 56), A("wv", 48, 56), ALU.mult)
                turn(A("tr"), A("gt"))
                tt(A("nn", 24, 28), A("pn", 48, 52), A("pn", 52, 56), ALU.add)
            tt(A("wv", a, a + 4), A("tr", s, 64, 16), A("tr", 64 + s, 128, 16), ALU.is_le)
            tt(A("wv", a + 4, a + 8), A("tr", s, 64, 16), A("tr", 64 + s, 128, 16), ALU.is_gt)
            if s == 7:
                copy(A("nbu", 24, 28), A("nn", 24, 28))
                act(A("gf", 384, 448), A("win"), off=A("nbu", 24, 28))
                tt(A("pn", 56, 64), A("wv", 56, 64), A("tr", 15, 128, 16), ALU.mult)
                gap()
                tt(A("nn", 28, 32), A("pn", 56, 60), A("pn", 60, 64), ALU.add)
                gap()
                copy(A("na", 28, 32), A("nn", 28, 32))
                to_list(7)
                turn(A("tf", 384, 448), A("gf", 384, 448))
                gap()
                copy(A("na", 24, 28), A("tf", 392, 448, 16))
                to_list(6, "s")
                while todo:
                    gap()
                break
            gap()
            dif = A("ts0", 0, 128, 16) if s == 0 else A("tr", 8 + s, 128, 16)
            base = A("ts0", 8, 128, 16) if s == 0 else A("tr", 8, 128, 16)
            tt(A("pt"), A("wv", a, a + 8), dif, ALU.mult)
            gap()
            tt(A("nw", a, a + 8), A("pt"), base, ALU.add)
            gap()
            copy(A("ll"), A("nw", a, a + 8))
            if s in (1, 3, 5):
                todo.extend(choices(s - 1))

    n_in_b = 2 * len(topo.engines(nxt, core))
    n_in_r = 2 * len(topo.engines(prv, core))
    for r in range(ROUNDS):
        last = r == ROUNDS - 1
        arrive("ba%d" % r, n_in_b, [A("qc", C, E), A("sc", C, E)])
        score(6, 7, 288, 416, 32, False)
        pick(A("sn", 0, 480), A("ss"), A("lru", 0, 30))
        act(A("sn", 480, 832), A("ss"), off=A("lru", 30, 52))
        act(A("s2", C, E), P(7, 32, 128), AF.Abs)
        for h in range(8):
            dma("y" if h < 4 else "s", "rl", A("win", p=(16 * h, 16 * h + 8)), A("sn", p=(0, 128, 16)))
        if r == 0:
            unpack((2, 3, 4, 5), 0, 128, "ssss")
            unpack((0, 1, 2, 3), 128, 320, "ssss")
        unpack((2, 3, 4, 5), 288, 416, "ssss", 32)
        for k in range(2):
            iota(A("inv%d" % k), [[0, 432]], 0, base=320)
        growth()
        for t in (2, 3):
            act(A("mt", t, 1280, 4), A("vt", E * t, E * t + E), off=A("nl"))
        act(A("nr"), A("iw"), off=A("nl"))
        for t in (0, 1):
            pick(A("mt", t, 1280, 4), A("vt", E * t, E * t + E), A("nl"))
        copy(A("nlf"), A("nl"))
        quant("m", 0, 320, A("mt"))
        hb = (0, 1, 6, 7)
        for b in range(4):
            mm(hb[b], "w", 128 * b, "m", 0, 320)
        for b in range(4):
            act(A("tb", b, 1280, 4), P(hb[b], 0, 320), scale=0.03125)
        tt(A("eq"), A("nlf"), A("nr"), ALU.is_equal, off=A("cidx"))
        if last:
            dma("y", "ob", T.on[:, :], A("nr", p=(0, 128, 16)))
        scan(A("scn"), A("dsc"), A("eq"), ALU.mult, ALU.add)
        ts(A("dq"), A("scn", 15, 320, 16), 32.0, ALU.is_ge, A("q4", 0, 1), ALU.mult)
        tt(A("ad"), A("nlf"), A("dq"), ALU.max)
        copy(A("adr", 0, 40, 2), A("ad"))
        for c in range(9, -1, -1):
            if c == 6:
                quant("t", 0, 320, A("tb"))
                for b in range(4):
                    mm(2 + b, "e", 128 * b, "t", 0, 320)
                for b in range(4):
                    act(A("tt", 336 * b, 336 * b + 320), P(2 + b, 0, 320), scale=-1.0)
            for k in (1, 0):
                d = 10 * k + c
                put(A("inv%d" % k), A("adr", 2 * d, 2 * d + 1), A("iw", 16 * d, 16 * d + 16))

        def lists(lo, hi, out):
            for k in (1, 0):
                scan(A("dg%d" % k, lo, hi), A("dia", lo, hi), A("inv%d" % k, lo, hi), ALU.add, ALU.max)
            m = A("dm", lo // 16, hi // 16)
            tt(m, A("dg0", lo + 15, hi, 16), A("dg1", lo + 15, hi, 16), ALU.min)
            ts(A(out), m, A("hs", 0, 1), ALU.subtract)

        def minus(t):
            return A("tt", 336 * t, 336 * t + 336)
        lists(C, E, "ulb")
        for t in (2, 3):
            act(A("ub", t, 384, 4), minus(t), scale=-1.0, off=A("ulb"))
        for t in (0, 1):
            ts(A("ub", t, 384, 4), minus(t), -1.0, ALU.mult, off=A("ulb"))
        quant("r", 0, 128, A("ub"))
        send(nxt, "r", 0, H, 128, "ra%d" % r, "rtl")
        lists(0, C, "ul")
        for t in range(4):
            tt(A("xt", 384 + t, 1280, 4), minus(t), A("vt", E * t + H, E * t + C), ALU.add, off=A("ul", 6, 20))
        quant("c", 128, 320, A("xt", 512, 1280))
        for t in range(4):
            tt(A("xf", H * t, H * t + H), minus(t), A("vt", E * t, E * t + H), ALU.add, off=A("ul", 0, 6))
        if last:
            quant("v", 0, 128, A("vin"))
            mm(6, "v", 0, "c", 128, 320)
            act(A("ysb", 128, 320), P(6, 0, 192))
            dma("y", "ob", T.y[:, 128:320], A("ysb", 128, 320))
        else:
            score(6, 7, 128, 320)
            unpack((2, 3, 4, 5), 128, 320, "ssss")
        arrive("ra%d" % r, n_in_r, [A("qr", 128, 224), A("sr", 128, 224)])
        bb = (0, 1, 7, 6)
        for b in range(4):
            mm(bb[b], "e", 128 * b, "r", 96, 224)
        for b in range(4):
            tt(A("xt", b, 384, 4), A("xf", H * b, H * b + H), P(bb[b], 32, 128), ALU.subtract)
        quant("c", 0, 128, A("xt", 0, 512))
        if last:
            mm(0, "v", 0, "c", 0, 128)
            act(A("ysb", 0, 128), P(0, 0, 128))
            dma("y", "ob", T.oc[:, :], A("qc", 0, 320, bits=dt.uint8))
            for k in range(4):
                dma("y" if k % 2 else "s", "ob", T.osc[4 * k:4 * k + 4, 0:320], A("sc", 0, 320, p=(32 * k, 32 * k + 4)))
            dma("s", "ob", T.y[:, 0:128], A("ysb", 0, 128))
        else:
            border_out(r + 1)
            score(0, 1, 0, 128)
            unpack((2, 3, 4, 5), 0, 128, "vvss")
    for s in SEMAPHORES:
        if know["g"].get(s, 0) < cnt[s]:
            g.wait_ge(T.sem[s], cnt[s])
